import numpy as np
import ml_dtypes


def mxq(x, axis, fmt="e4m3"):
    dtype, down = {"e4m3": (ml_dtypes.float8_e4m3fn, 7), "e5m2": (ml_dtypes.float8_e5m2, 14)}[fmt]
    v = np.moveaxis(np.asarray(x, np.float32).astype(ml_dtypes.bfloat16).astype(np.float64), axis, -1)
    blocks = v.reshape(v.shape[:-1] + (-1, 32))
    amax = np.abs(blocks).max(-1, keepdims=True)
    byte = np.maximum(np.where(amax > 0, np.frexp(amax)[1] - 1 + 127, 0) - down, 1)
    scale = np.exp2(byte - 127.0)
    codes = (blocks / scale).astype(np.float32).astype(dtype).astype(np.float64)
    return np.moveaxis((codes * scale).reshape(v.shape), -1, axis)


WIDE = False


def mx_kscale(k):
    if not WIDE:
        return np.ones(k)
    levels = np.array([10, -10, 5, -5, 0])
    if k % 512:
        return np.exp2(np.random.permutation(np.resize(levels, k // 32))).repeat(32)
    a = np.empty((k // 512, 16))
    for p in range(k // 512):
        a[p, :8] = np.random.permutation(np.resize(levels, 8))
        for g in range(8):
            far = levels[np.abs(levels - a[p, g]) >= 10]
            a[p, g + 8] = far[np.random.randint(len(far))]
    return np.exp2(a.ravel()).repeat(32)


def f64(x):
    return np.asarray(x).astype(np.float64)


def striped(idx):
    return np.tile(idx.reshape(-1, 16).T, (8, 1)).astype(np.uint16)


def unstriped(offs):
    return offs[:16].T.reshape(-1).astype(np.int64)


E2M1 = np.array([0.0, 0.5, 1.0, 1.5, 2.0, 3.0, 4.0, 6.0, -0.0, -0.5, -1.0, -1.5, -2.0, -3.0, -4.0, -6.0])


def pack_weight(w, fmt):
    k, n = w.shape
    w = f64(np.asarray(w, np.float32).astype(ml_dtypes.bfloat16)).reshape(k // 32, 32, n)
    amax = np.abs(w).max(1)
    if fmt == "e4m3":
        byte = np.frexp(amax)[1] - 1 + 127 - 7
    else:
        mant, ex = np.frexp(amax / 6.0)
        byte = np.where(mant > 0.5, ex, ex - 1) + 127
    byte = np.clip(np.where(amax > 0, byte, 1), 1, 254)
    scaled = (w * np.exp2(127.0 - byte)[:, None, :]).reshape(k, n).astype(np.float32)
    by_word = np.ascontiguousarray(scaled.reshape(k // 512, 128, 4, n).transpose(0, 1, 3, 2))
    if fmt == "e4m3":
        words = by_word.astype(ml_dtypes.float8_e4m3fn).view(np.uint8)
    else:
        c = by_word.astype(ml_dtypes.float4_e2m1fn).view(np.uint8) & 0xF
        words = (c[..., 0::2] | (c[..., 1::2] << 4)).reshape(k // 512, 128, 2 * n)
    return np.ascontiguousarray(words), np.ascontiguousarray(byte.astype(np.uint8).reshape(k // 512, 16, n))


def unpack_weight(words, scales, fmt):
    g, _, n = scales.shape
    words = np.ascontiguousarray(words).reshape(g, 128, n, -1)
    if fmt == "e4m3":
        vals = words.view(ml_dtypes.float8_e4m3fn).astype(np.float64)
    else:
        nib = np.empty((g, 128, n, 4), np.uint8)
        nib[..., 0::2] = words & 0xF
        nib[..., 1::2] = words >> 4
        vals = E2M1[nib]
    vals = vals * np.repeat(np.exp2(scales.astype(np.float64) - 127.0), 8, axis=1)[..., None]
    return vals.transpose(0, 1, 3, 2).reshape(g * 512, n)


K, T, E, C, N = 512, 2560, 6, 256, 512


def by_expert(wq, xq):
    return np.concatenate([wq[e].T @ xq[:, e * C:(e + 1) * C] for e in range(E)], axis=1)


def setup_inputs():
    n = np.random.standard_normal
    s = mx_kscale(K)[:, None]
    w = [pack_weight(m, "e2m1") for m in n((E, K, N)) / np.sqrt(K) / s[None]]
    return {
        "xT": (n((K, T)) * s).astype(np.float32),
        "w_words": np.stack([m[0] for m in w]),
        "w_scales": np.stack([m[1] for m in w]),
        "gate": np.tile(np.random.uniform(0.2, 1.0, E * C), (N, 1)).astype(np.float32),
        "offs": striped(np.random.permutation(T)[:E * C]),
    }


def reference(xT, w_words, w_scales, gate, offs):
    idx = unstriped(offs)
    w = np.stack([unpack_weight(w_words[e], w_scales[e], "e2m1") for e in range(E)])
    xq = mxq(f64(xT)[:, idx], 0, "e4m3")
    y = by_expert(w, xq)
    out = np.zeros((N, T))
    out[:, idx] = f64(gate) * y
    return out

@@ -1,0 +1,112 @@
+import concourse.mybir as mybir
+
+K, T, E, C, N = 512, 2560, 6, 256, 512
+P = 128
+SLOTS = E * C
+FLOPS = 2 * K * N * SLOTS
+
+F32 = mybir.dt.float32
+BF16 = mybir.dt.bfloat16
+I32 = mybir.dt.int32
+U32 = mybir.dt.uint32
+U16 = mybir.dt.uint16
+U8 = mybir.dt.uint8
+FP8X4 = mybir.dt.float8_e4m3fn_x4
+FP4X4 = mybir.dt.float4_e2m1fn_x4
+MULT = mybir.AluOpType.mult
+
+WIDTHS = (512, 512, 512, 512, 256, 256)
+GROUP = 512
+NT = N // P
+
+
+def tile_moe_pln_lin_none_kernel(tc, xT, w_words, w_scales, gate, offs, out):
+    nc = tc.nc
+    with (
+        tc.tile_pool(name="held", bufs=1) as held,
+        tc.psum_pool(name="psum", bufs=8) as psum,
+    ):
+        offsets = held.tile([P, SLOTS // 16], U16, name="offsets")
+        codes = held.tile([P, T], U32, name="codes", align_bytes=64)
+        scales = held.tile([P, T], U8, name="scales", align_bytes=64)
+        words = held.tile([P, E, 2 * N], U8, name="words", align_bytes=64)
+        wplane = held.tile([P, E, N], U8, name="wplane", align_bytes=64)
+        windows = [held.tile([P, T], F32, name=f"window{t}") for t in range(NT)]
+        gates = [held.tile([P, SLOTS], F32, name=f"gate{t}") for t in range(NT)]
+        results = [held.tile([P, SLOTS], F32, name=f"result{t}") for t in range(NT)]
+
+        nc.gpsimd.memset(scales[:].bitcast(I32), 0)
+        nc.gpsimd.memset(wplane[:].rearrange("p e n -> p (e n)").bitcast(I32), 0)
+
+        x_rows = xT.rearrange("(p j) w -> p j w", j=4)
+        raws, rounded = [], []
+        first = 0
+        for i, width in enumerate(WIDTHS):
+            raw = held.tile([P, 4, width], F32, name=f"raw{i}")
+            nc.sync.dma_start(raw[:], x_rows[:, :, first : first + width])
+            raws.append(raw)
+            rounded.append(held.tile([P, width, 4], BF16, name=f"rounded{i}", align_bytes=64))
+            first += width
+        nc.sync.dma_start(offsets[:], offs)
+        nc.sync.dma_start(
+            words[:].rearrange("p e b -> p (e b)").bitcast(I32).rearrange("p (e b) -> p e b", e=E),
+            w_words.bitcast(I32).rearrange("e a p b -> p (e a) b"),
+        )
+        plane_words = wplane[:].rearrange("p e n -> p (e n)").bitcast(I32).rearrange("p (e n) -> p e n", e=E)
+        scale_rows = w_scales.bitcast(I32).rearrange("e a q n -> q (e a) n")
+        for quad in range(4):
+            nc.sync.dma_start(plane_words[32 * quad : 32 * quad + 4], scale_rows[4 * quad : 4 * quad + 4])
+        for t in range(NT):
+            nc.sync.dma_start(gates[t][:], gate[P * t : P * (t + 1), :])
+
+        for t in range(NT):
+            nc.vector.memset(windows[t][:], 0.0)
+
+        first = 0
+        for i, width in enumerate(WIDTHS):
+            cut = width * 5 // 8
+            src = raws[i][:].rearrange("p j w -> p w j")
+            nc.scalar.copy(rounded[i][:, cut:, :], src[:, cut:, :])
+            nc.vector.tensor_copy(rounded[i][:, :cut, :], src[:, :cut, :])
+            nc.vector.quantize_mx(
+                out=codes[:, first : first + width].bitcast(FP8X4),
+                scales=scales[:, first : first + width],
+                in_=rounded[i][:].rearrange("p w j -> p (w j)"),
+            )
+            first += width
+
+        for g in range(SLOTS // GROUP):
+            slots = slice(g * GROUP, (g + 1) * GROUP)
+            listed = offsets[:, g * GROUP // 16 : (g + 1) * GROUP // 16]
+            slot_codes = held.tile([P, GROUP], U32, name=f"slot_codes{g}", align_bytes=64)
+            slot_scales = held.tile([P, GROUP], U8, name=f"slot_scales{g}", align_bytes=64)
+            nc.vector.tensor_copy(slot_codes[:], codes[:].indirect(listed))
+            nc.vector.tensor_copy(slot_scales[:], scales[:].indirect(listed))
+            for t in range(NT):
+                bank = psum.tile([P, GROUP], F32, name="bank")
+                for half in range(GROUP // C):
+                    e = g * GROUP // C + half
+                    cols = slice(half * C, (half + 1) * C)
+                    nc.tensor.matmul_mx(
+                        out=bank[:, cols],
+                        lhsT=words[:, e, 2 * P * t : 2 * P * (t + 1)].bitcast(FP4X4),
+                        lhsT_scale=wplane[:, e, P * t : P * (t + 1)],
+                        rhs=slot_codes[:, cols].bitcast(FP8X4),
+                        rhs_scale=slot_scales[:, cols],
+                        start=True,
+                        stop=True,
+                    )
+                nc.scalar.copy(results[t][:, slots], bank[:])
+
+        for t in range(NT):
+            pieces = [(g * GROUP, (g + 1) * GROUP) for g in range(SLOTS // GROUP)] if t == 0 else [(0, SLOTS)]
+            for a, b in pieces:
+                nc.vector.tensor_tensor(
+                    windows[t][:].indirect(offsets[:, a // 16 : b // 16]),
+                    results[t][:, a:b],
+                    gates[t][:, a:b],
+                    MULT,
+                )
+            half = T // 2
+            nc.sync.dma_start(out[P * t : P * (t + 1), :half], windows[t][:, :half])
+            nc.scalar.dma_start(out[P * t : P * (t + 1), half:], windows[t][:, half:])

@@ -14,10 +14,13 @@ U8 = mybir.dt.uint8
 FP8X4 = mybir.dt.float8_e4m3fn_x4
 FP4X4 = mybir.dt.float4_e2m1fn_x4
 MULT = mybir.AluOpType.mult
+COPY = mybir.ActivationFunctionType.Copy
 
-WIDTHS = (512, 512, 512, 512, 256, 256)
-GROUP = 512
 NT = N // P
+BANK = 512
+EARLY = 512
+LATE = SLOTS - EARLY
+WINDOWS = 3
 
 
 def tile_moe_pln_lin_none_kernel(tc, xT, w_words, w_scales, gate, offs, out):
@@ -27,86 +30,112 @@ def tile_moe_pln_lin_none_kernel(tc, xT, w_words, w_scales, gate, offs, out):
         tc.psum_pool(name="psum", bufs=8) as psum,
     ):
         offsets = held.tile([P, SLOTS // 16], U16, name="offsets")
-        codes = held.tile([P, T], U32, name="codes", align_bytes=64)
-        scales = held.tile([P, T], U8, name="scales", align_bytes=64)
-        words = held.tile([P, E, 2 * N], U8, name="words", align_bytes=64)
         wplane = held.tile([P, E, N], U8, name="wplane", align_bytes=64)
-        windows = [held.tile([P, T], F32, name=f"window{t}") for t in range(NT)]
-        gates = [held.tile([P, SLOTS], F32, name=f"gate{t}") for t in range(NT)]
-        results = [held.tile([P, SLOTS], F32, name=f"result{t}") for t in range(NT)]
+        windows = [held.tile([P, T], F32, name=f"window{t}") for t in range(WINDOWS)]
+        early_list = offsets[:, : EARLY // 16]
+        late_list = offsets[:, EARLY // 16 :]
+        early_experts = EARLY // C
 
-        nc.gpsimd.memset(scales[:].bitcast(I32), 0)
-        nc.gpsimd.memset(wplane[:].rearrange("p e n -> p (e n)").bitcast(I32), 0)
+        nc.vector.memset(wplane[:].rearrange("p e n -> p (e n)").bitcast(I32), 0)
+        nc.vector.memset(windows[0][:], 0.0)
+        nc.vector.memset(windows[1][:], 0.0)
+        nc.scalar.activation(windows[2][:], windows[0][:], COPY)
 
         x_rows = xT.rearrange("(p j) w -> p j w", j=4)
-        raws, rounded = [], []
-        first = 0
-        for i, width in enumerate(WIDTHS):
-            raw = held.tile([P, 4, width], F32, name=f"raw{i}")
-            nc.sync.dma_start(raw[:], x_rows[:, :, first : first + width])
+        raws = []
+        for j in range(4):
+            raw = held.tile([P, T], F32, name=f"raw{j}", tag=f"raw{j}", align_bytes=64)
+            nc.sync.dma_start(raw[:], x_rows[:, j, :])
             raws.append(raw)
-            rounded.append(held.tile([P, width, 4], BF16, name=f"rounded{i}", align_bytes=64))
-            first += width
-        nc.sync.dma_start(offsets[:], offs)
-        nc.sync.dma_start(
-            words[:].rearrange("p e b -> p (e b)").bitcast(I32).rearrange("p (e b) -> p e b", e=E),
-            w_words.bitcast(I32).rearrange("e a p b -> p (e a) b"),
-        )
+            if j == 0:
+                nc.sync.dma_start(offsets[:], offs)
+
+        def load_words(tile, first, last):
+            nc.sync.dma_start(
+                tile[:].rearrange("p e b -> p (e b)").bitcast(I32).rearrange("p (e b) -> p e b", e=last - first),
+                w_words[first:last].bitcast(I32).rearrange("e a p b -> p (e a) b"),
+            )
+
+        early_words = held.tile([P, early_experts, 2 * N], U8, name="early_words", align_bytes=64)
+        load_words(early_words, 0, early_experts)
         plane_words = wplane[:].rearrange("p e n -> p (e n)").bitcast(I32).rearrange("p (e n) -> p e n", e=E)
         scale_rows = w_scales.bitcast(I32).rearrange("e a q n -> q (e a) n")
         for quad in range(4):
             nc.sync.dma_start(plane_words[32 * quad : 32 * quad + 4], scale_rows[4 * quad : 4 * quad + 4])
-        for t in range(NT):
-            nc.sync.dma_start(gates[t][:], gate[P * t : P * (t + 1), :])
 
-        for t in range(NT):
-            nc.vector.memset(windows[t][:], 0.0)
+        early_in = held.tile([P, EARLY, 4], BF16, name="early_in", tag="early_in", align_bytes=64)
+        late_in = held.tile([P, LATE, 4], BF16, name="late_in", align_bytes=64)
+        for j in range(3):
+            plane = held.tile([P, T], BF16, name=f"plane{j}")
+            nc.vector.tensor_copy(plane[:], raws[j][:])
+            nc.vector.tensor_copy(early_in[:, :, j], raws[j][:].indirect(early_list))
+            nc.scalar.activation(late_in[:, :, j], plane[:].indirect(late_list), COPY)
 
-        first = 0
-        for i, width in enumerate(WIDTHS):
-            cut = width * 5 // 8
-            src = raws[i][:].rearrange("p j w -> p w j")
-            nc.scalar.copy(rounded[i][:, cut:, :], src[:, cut:, :])
-            nc.vector.tensor_copy(rounded[i][:, :cut, :], src[:, :cut, :])
-            nc.vector.quantize_mx(
-                out=codes[:, first : first + width].bitcast(FP8X4),
-                scales=scales[:, first : first + width],
-                in_=rounded[i][:].rearrange("p w j -> p (w j)"),
-            )
-            first += width
+        gates = held.tile([P, SLOTS], F32, name="gates", tag="raw0", align_bytes=64)
+        nc.sync.dma_start(gates[:, :EARLY], gate[:P, :EARLY])
+        nc.sync.dma_start(gates[:, EARLY:], gate[:P, EARLY:])
+        late_words = held.tile([P, E - early_experts, 2 * N], U8, name="late_words", tag="raw1", align_bytes=64)
+        load_words(late_words, early_experts, E)
 
-        for g in range(SLOTS // GROUP):
-            slots = slice(g * GROUP, (g + 1) * GROUP)
-            listed = offsets[:, g * GROUP // 16 : (g + 1) * GROUP // 16]
-            slot_codes = held.tile([P, GROUP], U32, name=f"slot_codes{g}", align_bytes=64)
-            slot_scales = held.tile([P, GROUP], U8, name=f"slot_scales{g}", align_bytes=64)
-            nc.vector.tensor_copy(slot_codes[:], codes[:].indirect(listed))
-            nc.vector.tensor_copy(slot_scales[:], scales[:].indirect(listed))
-            for t in range(NT):
-                bank = psum.tile([P, GROUP], F32, name="bank")
-                for half in range(GROUP // C):
-                    e = g * GROUP // C + half
-                    cols = slice(half * C, (half + 1) * C)
+        def products(codes, scales, words, first_expert, t, result, count, copy):
+            for start in range(0, count, BANK):
+                bank = psum.tile([P, BANK], F32, name="bank")
+                for half in range(BANK // C):
+                    e = start // C + half
                     nc.tensor.matmul_mx(
-                        out=bank[:, cols],
+                        out=bank[:, half * C : (half + 1) * C],
                         lhsT=words[:, e, 2 * P * t : 2 * P * (t + 1)].bitcast(FP4X4),
-                        lhsT_scale=wplane[:, e, P * t : P * (t + 1)],
-                        rhs=slot_codes[:, cols].bitcast(FP8X4),
-                        rhs_scale=slot_scales[:, cols],
+                        lhsT_scale=wplane[:, first_expert + e, P * t : P * (t + 1)],
+                        rhs=codes[:, e * C : (e + 1) * C].bitcast(FP8X4),
+                        rhs_scale=scales[:, e * C : (e + 1) * C],
                         start=True,
                         stop=True,
                     )
-                nc.scalar.copy(results[t][:, slots], bank[:])
+                copy(result[:, start : start + BANK], bank[:])
 
-        for t in range(NT):
-            pieces = [(g * GROUP, (g + 1) * GROUP) for g in range(SLOTS // GROUP)] if t == 0 else [(0, SLOTS)]
-            for a, b in pieces:
-                nc.vector.tensor_tensor(
-                    windows[t][:].indirect(offsets[:, a // 16 : b // 16]),
-                    results[t][:, a:b],
-                    gates[t][:, a:b],
-                    MULT,
-                )
-            half = T // 2
-            nc.sync.dma_start(out[P * t : P * (t + 1), :half], windows[t][:, :half])
-            nc.scalar.dma_start(out[P * t : P * (t + 1), half:], windows[t][:, half:])
+        nc.vector.tensor_copy(early_in[:, :, 3], raws[3][:].indirect(early_list))
+        early_codes = held.tile([P, EARLY], U32, name="early_codes", align_bytes=64)
+        early_scales = held.tile([P, EARLY], U8, name="early_scales", align_bytes=64)
+        nc.vector.quantize_mx(
+            out=early_codes[:].bitcast(FP8X4),
+            scales=early_scales[:],
+            in_=early_in[:].rearrange("p w j -> p (w j)"),
+        )
+        plane = held.tile([P, T], BF16, name="plane3", tag="early_in", align_bytes=64)
+        nc.vector.tensor_copy(plane[:], raws[3][:])
+
+        last = held.tile([P, SLOTS], F32, name="last_result")
+        early_results = [
+            held.tile([P, EARLY], F32, name=f"early_result{t}", tag=f"early_result{t}", align_bytes=64)
+            for t in range(WINDOWS)
+        ]
+        products(early_codes, early_scales, early_words, 0, 0, early_results[0], EARLY, nc.vector.tensor_copy)
+        products(early_codes, early_scales, early_words, 0, 1, early_results[1], EARLY, nc.scalar.copy)
+        nc.scalar.activation(late_in[:, :, 3], plane[:].indirect(late_list), COPY)
+        products(early_codes, early_scales, early_words, 0, 2, early_results[2], EARLY, nc.scalar.copy)
+        products(early_codes, early_scales, early_words, 0, 3, last[:, :EARLY], EARLY, nc.scalar.copy)
+
+        for t in range(2):
+            nc.vector.tensor_tensor(windows[t][:].indirect(early_list), early_results[t][:], gates[:, :EARLY], MULT)
+
+        late_codes = held.tile([P, LATE], U32, name="late_codes", tag="early_result0", align_bytes=64)
+        late_scales = held.tile([P, LATE], U8, name="late_scales", align_bytes=64)
+        nc.vector.quantize_mx(
+            out=late_codes[:].bitcast(FP8X4),
+            scales=late_scales[:],
+            in_=late_in[:].rearrange("p w j -> p (w j)"),
+        )
+        nc.vector.tensor_tensor(windows[2][:].indirect(early_list), early_results[2][:], gates[:, :EARLY], MULT)
+
+        late_results = [held.tile([P, LATE], F32, name=f"late_result{t}") for t in range(WINDOWS)]
+        for t in range(WINDOWS):
+            products(late_codes, late_scales, late_words, early_experts, t, late_results[t], LATE, nc.scalar.copy)
+        products(late_codes, late_scales, late_words, early_experts, 3, last[:, EARLY:], LATE, nc.scalar.copy)
+
+        for t in range(WINDOWS):
+            nc.vector.tensor_tensor(windows[t][:].indirect(late_list), late_results[t][:], gates[:, EARLY:], MULT)
+            nc.sync.dma_start(out[P * t : P * (t + 1), :], windows[t][:])
+        nc.vector.tensor_tensor(windows[0][:].indirect(offsets[:]), last[:], gates[:], MULT)
+        half = T // 2
+        nc.sync.dma_start(out[P * 3 :, :half], windows[0][:, :half])
+        nc.scalar.dma_start(out[P * 3 :, half:], windows[0][:, half:])

@@ -94,48 +94,48 @@ def tile_moe_pln_lin_none_kernel(tc, xT, w_words, w_scales, gate, offs, out):
                 copy(result[:, start : start + BANK], bank[:])
 
         nc.vector.tensor_copy(early_in[:, :, 3], raws[3][:].indirect(early_list))
-        early_codes = held.tile([P, EARLY], U32, name="early_codes", align_bytes=64)
+        early_codes = held.tile([P, EARLY], U32, name="early_codes", tag="early_codes", align_bytes=64)
         early_scales = held.tile([P, EARLY], U8, name="early_scales", align_bytes=64)
         nc.vector.quantize_mx(
             out=early_codes[:].bitcast(FP8X4),
             scales=early_scales[:],
             in_=early_in[:].rearrange("p w j -> p (w j)"),
         )
-        plane = held.tile([P, T], BF16, name="plane3", tag="early_in", align_bytes=64)
-        nc.vector.tensor_copy(plane[:], raws[3][:])
-
-        last = held.tile([P, SLOTS], F32, name="last_result")
+        windows.append(held.tile([P, T], F32, name="window3", tag="raw2", align_bytes=64))
+        nc.sync.dma_start(windows[3][:], windows[2][:])
         early_results = [
             held.tile([P, EARLY], F32, name=f"early_result{t}", tag=f"early_result{t}", align_bytes=64)
-            for t in range(WINDOWS)
+            for t in range(NT)
         ]
-        products(early_codes, early_scales, early_words, 0, 0, early_results[0], EARLY, nc.vector.tensor_copy)
-        products(early_codes, early_scales, early_words, 0, 1, early_results[1], EARLY, nc.scalar.copy)
-        nc.scalar.activation(late_in[:, :, 3], plane[:].indirect(late_list), COPY)
-        products(early_codes, early_scales, early_words, 0, 2, early_results[2], EARLY, nc.scalar.copy)
-        products(early_codes, early_scales, early_words, 0, 3, last[:, :EARLY], EARLY, nc.scalar.copy)
+        for t in range(NT):
+            copy = nc.vector.tensor_copy if t == 0 else nc.scalar.copy
+            products(early_codes, early_scales, early_words, 0, t, early_results[t], EARLY, copy)
 
-        for t in range(2):
+        plane = held.tile([P, T], BF16, name="plane3", tag="early_codes", align_bytes=64)
+        nc.scalar.activation(plane[:], raws[3][:], COPY)
+        nc.scalar.activation(late_in[:, :, 3], plane[:].indirect(late_list), COPY)
+
+        def scatter_early(t):
             nc.vector.tensor_tensor(windows[t][:].indirect(early_list), early_results[t][:], gates[:, :EARLY], MULT)
 
-        late_codes = held.tile([P, LATE], U32, name="late_codes", tag="early_result0", align_bytes=64)
+        for t in range(NT - 1):
+            scatter_early(t)
+        late_codes = held.tile([P, LATE], U32, name="late_codes", tag="early_result1", align_bytes=64)
         late_scales = held.tile([P, LATE], U8, name="late_scales", align_bytes=64)
         nc.vector.quantize_mx(
             out=late_codes[:].bitcast(FP8X4),
             scales=late_scales[:],
             in_=late_in[:].rearrange("p w j -> p (w j)"),
         )
-        nc.vector.tensor_tensor(windows[2][:].indirect(early_list), early_results[2][:], gates[:, :EARLY], MULT)
+        scatter_early(NT - 1)
 
-        late_results = [held.tile([P, LATE], F32, name=f"late_result{t}") for t in range(WINDOWS)]
-        for t in range(WINDOWS):
-            products(late_codes, late_scales, late_words, early_experts, t, late_results[t], LATE, nc.scalar.copy)
-        products(late_codes, late_scales, late_words, early_experts, 3, last[:, EARLY:], LATE, nc.scalar.copy)
-
-        for t in range(WINDOWS):
-            nc.vector.tensor_tensor(windows[t][:].indirect(late_list), late_results[t][:], gates[:, EARLY:], MULT)
-            nc.sync.dma_start(out[P * t : P * (t + 1), :], windows[t][:])
-        nc.vector.tensor_tensor(windows[0][:].indirect(offsets[:]), last[:], gates[:], MULT)
         half = T // 2
-        nc.sync.dma_start(out[P * 3 :, :half], windows[0][:, :half])
-        nc.scalar.dma_start(out[P * 3 :, half:], windows[0][:, half:])
+        for t in range(NT):
+            late_result = held.tile([P, LATE], F32, name=f"late_result{t}")
+            products(late_codes, late_scales, late_words, early_experts, t, late_result, LATE, nc.scalar.copy)
+            nc.vector.tensor_tensor(windows[t][:].indirect(late_list), late_result[:], gates[:, EARLY:], MULT)
+            if t < NT - 1:
+                nc.sync.dma_start(out[P * t : P * (t + 1), :], windows[t][:])
+            else:
+                nc.sync.dma_start(out[P * t :, :half], windows[t][:, :half])
+                nc.scalar.dma_start(out[P * t :, half:], windows[t][:, half:])

@@ -20,7 +20,6 @@ NT = N // P
 BANK = 512
 EARLY = 512
 LATE = SLOTS - EARLY
-WINDOWS = 3
 
 
 def tile_moe_pln_lin_none_kernel(tc, xT, w_words, w_scales, gate, offs, out):
@@ -31,15 +30,15 @@ def tile_moe_pln_lin_none_kernel(tc, xT, w_words, w_scales, gate, offs, out):
     ):
         offsets = held.tile([P, SLOTS // 16], U16, name="offsets")
         wplane = held.tile([P, E, N], U8, name="wplane", align_bytes=64)
-        windows = [held.tile([P, T], F32, name=f"window{t}") for t in range(WINDOWS)]
+        windows = [held.tile([P, T], F32, name=f"window{t}") for t in range(NT)]
         early_list = offsets[:, : EARLY // 16]
         late_list = offsets[:, EARLY // 16 :]
         early_experts = EARLY // C
 
         nc.vector.memset(wplane[:].rearrange("p e n -> p (e n)").bitcast(I32), 0)
-        nc.vector.memset(windows[0][:], 0.0)
-        nc.vector.memset(windows[1][:], 0.0)
-        nc.scalar.activation(windows[2][:], windows[0][:], COPY)
+        for t in range(NT - 1):
+            nc.vector.memset(windows[t][:].bitcast(I32), 0)
+        nc.scalar.activation(windows[NT - 1][:], windows[0][:], COPY)
 
         x_rows = xT.rearrange("(p j) w -> p j w", j=4)
         raws = []
@@ -67,8 +66,13 @@ def tile_moe_pln_lin_none_kernel(tc, xT, w_words, w_scales, gate, offs, out):
         late_in = held.tile([P, LATE, 4], BF16, name="late_in", align_bytes=64)
         for j in range(3):
             plane = held.tile([P, T], BF16, name=f"plane{j}")
-            nc.vector.tensor_copy(plane[:], raws[j][:])
-            nc.vector.tensor_copy(early_in[:, :, j], raws[j][:].indirect(early_list))
+            if j < 2:
+                nc.vector.tensor_copy(plane[:], raws[j][:])
+                nc.vector.tensor_copy(early_in[:, :, j], raws[j][:].indirect(early_list))
+            else:
+                nc.vector.tensor_copy(early_in[:, :, j], raws[j][:].indirect(early_list))
+                nc.vector.tensor_copy(plane[:, : T // 2], raws[j][:, : T // 2])
+                nc.scalar.activation(plane[:, T // 2 :], raws[j][:, T // 2 :], COPY)
             nc.scalar.activation(late_in[:, :, j], plane[:].indirect(late_list), COPY)
 
         gates = held.tile([P, SLOTS], F32, name="gates", tag="raw0", align_bytes=64)
@@ -77,43 +81,50 @@ def tile_moe_pln_lin_none_kernel(tc, xT, w_words, w_scales, gate, offs, out):
         late_words = held.tile([P, E - early_experts, 2 * N], U8, name="late_words", tag="raw1", align_bytes=64)
         load_words(late_words, early_experts, E)
 
-        def products(codes, scales, words, first_expert, t, result, count, copy):
-            for start in range(0, count, BANK):
-                bank = psum.tile([P, BANK], F32, name="bank")
-                for half in range(BANK // C):
-                    e = start // C + half
-                    nc.tensor.matmul_mx(
-                        out=bank[:, half * C : (half + 1) * C],
-                        lhsT=words[:, e, 2 * P * t : 2 * P * (t + 1)].bitcast(FP4X4),
-                        lhsT_scale=wplane[:, first_expert + e, P * t : P * (t + 1)],
-                        rhs=codes[:, e * C : (e + 1) * C].bitcast(FP8X4),
-                        rhs_scale=scales[:, e * C : (e + 1) * C],
-                        start=True,
-                        stop=True,
-                    )
-                copy(result[:, start : start + BANK], bank[:])
+        def fill_bank(codes, scales, words, first_expert, t, start, width):
+            bank = psum.tile([P, width], F32, name="bank")
+            for half in range(width // C):
+                e = start // C + half
+                nc.tensor.matmul_mx(
+                    out=bank[:, half * C : (half + 1) * C],
+                    lhsT=words[:, e, 2 * P * t : 2 * P * (t + 1)].bitcast(FP4X4),
+                    lhsT_scale=wplane[:, first_expert + e, P * t : P * (t + 1)],
+                    rhs=codes[:, e * C : (e + 1) * C].bitcast(FP8X4),
+                    rhs_scale=scales[:, e * C : (e + 1) * C],
+                    start=True,
+                    stop=True,
+                )
+            return bank
+
+        def products(codes, scales, words, first_expert, t, result, count, copy, width=BANK):
+            for start in range(0, count, width):
+                bank = fill_bank(codes, scales, words, first_expert, t, start, width)
+                copy(result[:, start : start + width], bank[:])
 
         nc.vector.tensor_copy(early_in[:, :, 3], raws[3][:].indirect(early_list))
         early_codes = held.tile([P, EARLY], U32, name="early_codes", tag="early_codes", align_bytes=64)
         early_scales = held.tile([P, EARLY], U8, name="early_scales", align_bytes=64)
-        nc.vector.quantize_mx(
-            out=early_codes[:].bitcast(FP8X4),
-            scales=early_scales[:],
-            in_=early_in[:].rearrange("p w j -> p (w j)"),
-        )
-        windows.append(held.tile([P, T], F32, name="window3", tag="raw2", align_bytes=64))
-        nc.sync.dma_start(windows[3][:], windows[2][:])
+        for e in range(early_experts):
+            cols = slice(e * C, (e + 1) * C)
+            nc.vector.quantize_mx(
+                out=early_codes[:, cols].bitcast(FP8X4),
+                scales=early_scales[:, cols],
+                in_=early_in[:, cols, :].rearrange("p w j -> p (w j)"),
+            )
         early_results = [
             held.tile([P, EARLY], F32, name=f"early_result{t}", tag=f"early_result{t}", align_bytes=64)
-            for t in range(NT)
+            for t in range(NT - 1)
         ]
-        for t in range(NT):
-            copy = nc.vector.tensor_copy if t == 0 else nc.scalar.copy
-            products(early_codes, early_scales, early_words, 0, t, early_results[t], EARLY, copy)
+        products(early_codes, early_scales, early_words, 0, 0, early_results[0], EARLY, nc.vector.tensor_copy, C)
+        for t in range(1, NT - 1):
+            products(early_codes, early_scales, early_words, 0, t, early_results[t], EARLY, nc.scalar.copy)
+        last_bank = fill_bank(early_codes, early_scales, early_words, 0, NT - 1, 0, EARLY)
 
         plane = held.tile([P, T], BF16, name="plane3", tag="early_codes", align_bytes=64)
         nc.scalar.activation(plane[:], raws[3][:], COPY)
         nc.scalar.activation(late_in[:, :, 3], plane[:].indirect(late_list), COPY)
+        early_results.append(held.tile([P, EARLY], F32, name="early_result3", tag="early_codes", align_bytes=64))
+        nc.scalar.copy(early_results[NT - 1][:], last_bank[:])
 
         def scatter_early(t):
             nc.vector.tensor_tensor(windows[t][:].indirect(early_list), early_results[t][:], gates[:, :EARLY], MULT)

@@ -20,6 +20,7 @@ NT = N // P
 BANK = 512
 EARLY = 512
 LATE = SLOTS - EARLY
+VECTOR_ROUNDS = (T * 5 // 8, T, T // 4)
 
 
 def tile_moe_pln_lin_none_kernel(tc, xT, w_words, w_scales, gate, offs, out):
@@ -66,13 +67,14 @@ def tile_moe_pln_lin_none_kernel(tc, xT, w_words, w_scales, gate, offs, out):
         late_in = held.tile([P, LATE, 4], BF16, name="late_in", align_bytes=64)
         for j in range(3):
             plane = held.tile([P, T], BF16, name=f"plane{j}")
+            cut = VECTOR_ROUNDS[j]
+            if j == 2:
+                nc.vector.tensor_copy(early_in[:, :, j], raws[j][:].indirect(early_list))
+            nc.vector.tensor_copy(plane[:, :cut], raws[j][:, :cut])
+            if cut < T:
+                nc.scalar.activation(plane[:, cut:], raws[j][:, cut:], COPY)
             if j < 2:
-                nc.vector.tensor_copy(plane[:], raws[j][:])
                 nc.vector.tensor_copy(early_in[:, :, j], raws[j][:].indirect(early_list))
-            else:
-                nc.vector.tensor_copy(early_in[:, :, j], raws[j][:].indirect(early_list))
-                nc.vector.tensor_copy(plane[:, : T // 2], raws[j][:, : T // 2])
-                nc.scalar.activation(plane[:, T // 2 :], raws[j][:, T // 2 :], COPY)
             nc.scalar.activation(late_in[:, :, j], plane[:].indirect(late_list), COPY)
 
         gates = held.tile([P, SLOTS], F32, name="gates", tag="raw0", align_bytes=64)

@@ -17,10 +17,12 @@ MULT = mybir.AluOpType.mult
 COPY = mybir.ActivationFunctionType.Copy
 
 NT = N // P
-BANK = 512
-EARLY = 512
-LATE = SLOTS - EARLY
-VECTOR_ROUNDS = (T * 5 // 8, T, T // 4)
+ADD = mybir.AluOpType.add
+GROUP = 512
+HALF = T // 2
+VECTOR_ROUNDS = 1664
+VECTOR_ROUNDS_LAST = 384
+MIN_STEPPED = T // 8
 
 
 def tile_moe_pln_lin_none_kernel(tc, xT, w_words, w_scales, gate, offs, out):
@@ -29,126 +31,196 @@ def tile_moe_pln_lin_none_kernel(tc, xT, w_words, w_scales, gate, offs, out):
         tc.tile_pool(name="held", bufs=1) as held,
         tc.psum_pool(name="psum", bufs=8) as psum,
     ):
+        def tile(shape, dtype, name, tag=None):
+            return held.tile(shape, dtype, name=name, tag=tag or name, align_bytes=64)
+
         offsets = held.tile([P, SLOTS // 16], U16, name="offsets")
-        wplane = held.tile([P, E, N], U8, name="wplane", align_bytes=64)
-        windows = [held.tile([P, T], F32, name=f"window{t}") for t in range(NT)]
-        early_list = offsets[:, : EARLY // 16]
-        late_list = offsets[:, EARLY // 16 :]
-        early_experts = EARLY // C
+
+        def listed(first, last):
+            return offsets[:, first // 16 : last // 16]
+
+        wplane = tile([P, E, N], U8, "wplane")
+        windows = [tile([P, T], F32, f"window{t}") for t in range(2)]
 
         nc.vector.memset(wplane[:].rearrange("p e n -> p (e n)").bitcast(I32), 0)
-        for t in range(NT - 1):
-            nc.vector.memset(windows[t][:].bitcast(I32), 0)
-        nc.scalar.activation(windows[NT - 1][:], windows[0][:], COPY)
+        zeros = windows[0][:, :HALF]
+        nc.vector.memset(zeros.bitcast(I32), 0)
+        nc.scalar.activation(windows[1][:, HALF:], zeros, COPY)
+        nc.vector.tensor_copy(windows[0][:, HALF:], zeros)
+        nc.vector.tensor_copy(windows[1][:, :HALF], zeros)
+        nothing = tile([P, C], F32, "nothing")
+        nc.vector.memset(nothing[:].bitcast(I32), 0)
 
         x_rows = xT.rearrange("(p j) w -> p j w", j=4)
         raws = []
         for j in range(4):
-            raw = held.tile([P, T], F32, name=f"raw{j}", tag=f"raw{j}", align_bytes=64)
+            raw = tile([P, T], F32, f"raw{j}")
             nc.sync.dma_start(raw[:], x_rows[:, j, :])
             raws.append(raw)
             if j == 0:
                 nc.sync.dma_start(offsets[:], offs)
 
-        def load_words(tile, first, last):
-            nc.sync.dma_start(
-                tile[:].rearrange("p e b -> p (e b)").bitcast(I32).rearrange("p (e b) -> p e b", e=last - first),
-                w_words[first:last].bitcast(I32).rearrange("e a p b -> p (e a) b"),
-            )
-
-        early_words = held.tile([P, early_experts, 2 * N], U8, name="early_words", align_bytes=64)
-        load_words(early_words, 0, early_experts)
+        gates = tile([P, SLOTS], F32, "gates")
+        nc.sync.dma_start(gates[:, :C], gate[:P, :C])
+        word_rows = w_words.bitcast(I32).rearrange("e a p b -> p (e a) b")
+        block = 2 * P
+        first_words = tile([P, 3 * block], U8, "first_words", "chain")
+        nc.sync.dma_start(first_words[:].bitcast(I32), word_rows[:, 0, : 3 * block // 4])
         plane_words = wplane[:].rearrange("p e n -> p (e n)").bitcast(I32).rearrange("p (e n) -> p e n", e=E)
         scale_rows = w_scales.bitcast(I32).rearrange("e a q n -> q (e a) n")
-        for quad in range(4):
-            nc.sync.dma_start(plane_words[32 * quad : 32 * quad + 4], scale_rows[4 * quad : 4 * quad + 4])
 
-        early_in = held.tile([P, EARLY, 4], BF16, name="early_in", tag="early_in", align_bytes=64)
-        late_in = held.tile([P, LATE, 4], BF16, name="late_in", align_bytes=64)
-        for j in range(3):
-            plane = held.tile([P, T], BF16, name=f"plane{j}")
-            cut = VECTOR_ROUNDS[j]
-            if j == 2:
-                nc.vector.tensor_copy(early_in[:, :, j], raws[j][:].indirect(early_list))
-            nc.vector.tensor_copy(plane[:, :cut], raws[j][:, :cut])
-            if cut < T:
-                nc.scalar.activation(plane[:, cut:], raws[j][:, cut:], COPY)
-            if j < 2:
-                nc.vector.tensor_copy(early_in[:, :, j], raws[j][:].indirect(early_list))
-            nc.scalar.activation(late_in[:, :, j], plane[:].indirect(late_list), COPY)
-
-        gates = held.tile([P, SLOTS], F32, name="gates", tag="raw0", align_bytes=64)
-        nc.sync.dma_start(gates[:, :EARLY], gate[:P, :EARLY])
-        nc.sync.dma_start(gates[:, EARLY:], gate[:P, EARLY:])
-        late_words = held.tile([P, E - early_experts, 2 * N], U8, name="late_words", tag="raw1", align_bytes=64)
-        load_words(late_words, early_experts, E)
-
-        def fill_bank(codes, scales, words, first_expert, t, start, width):
-            bank = psum.tile([P, width], F32, name="bank")
-            for half in range(width // C):
-                e = start // C + half
-                nc.tensor.matmul_mx(
-                    out=bank[:, half * C : (half + 1) * C],
-                    lhsT=words[:, e, 2 * P * t : 2 * P * (t + 1)].bitcast(FP4X4),
-                    lhsT_scale=wplane[:, first_expert + e, P * t : P * (t + 1)],
-                    rhs=codes[:, e * C : (e + 1) * C].bitcast(FP8X4),
-                    rhs_scale=scales[:, e * C : (e + 1) * C],
-                    start=True,
-                    stop=True,
+        def load_scales(first, last):
+            for quad in range(4):
+                nc.sync.dma_start(
+                    plane_words[32 * quad : 32 * quad + 4, first:last], scale_rows[4 * quad : 4 * quad + 4, first:last]
                 )
+
+        load_scales(0, 2)
+        words1 = tile([P, 2 * N], U8, "words1")
+        nc.sync.dma_start(words1[:].bitcast(I32), word_rows[:, 1, :])
+        nc.sync.dma_start(gates[:, C:GROUP], gate[:P, C:GROUP])
+        words0 = tile([P, block], U8, "words0")
+        nc.sync.dma_start(words0[:].bitcast(I32), word_rows[:, 0, 3 * block // 4 :])
+
+        early_in = tile([P, GROUP, 4], BF16, "early_in")
+        pairs1 = tile([P, 2, GROUP, 2], BF16, "pairs1")
+        planes = []
+        for j in range(3):
+            plane = tile([P, T], BF16, f"plane{j}")
+            planes.append(plane)
+            nc.vector.tensor_copy(plane[:, :VECTOR_ROUNDS], raws[j][:, :VECTOR_ROUNDS])
+            nc.scalar.activation(plane[:, VECTOR_ROUNDS:], raws[j][:, VECTOR_ROUNDS:], COPY)
+            nc.vector.tensor_copy(early_in[:, :, j], raws[j][:].indirect(listed(0, GROUP)))
+            nc.scalar.activation(pairs1[:, j // 2, :, j % 2], plane[:].indirect(listed(GROUP, 2 * GROUP)), COPY)
+
+        def quantise(codes, scales, values):
+            nc.vector.quantize_mx(out=codes.bitcast(FP8X4), scales=scales, in_=values.rearrange("p w j -> p (w j)"))
+
+        def product(target, words, e, t, codes, scales):
+            nc.tensor.matmul_mx(
+                out=target,
+                lhsT=words.bitcast(FP4X4),
+                lhsT_scale=wplane[:, e, P * t : P * (t + 1)],
+                rhs=codes.bitcast(FP8X4),
+                rhs_scale=scales,
+                start=True,
+                stop=True,
+            )
+
+        pieces = [slice(P, 2 * P), slice(0, P)]
+        dense = [tile([P, P], BF16, f"dense{i}") for i in range(2)]
+        for piece, picked in zip(pieces, dense):
+            nc.vector.tensor_copy(picked[:], raws[3][:].indirect(listed(piece.start, piece.stop)))
+        for piece, picked in zip(pieces, dense):
+            nc.vector.tensor_copy(early_in[:, piece, 3], picked[:])
+        codes0 = tile([P, C], U32, "codes0")
+        scales0 = tile([P, C], U8, "scales0")
+        first_bank = psum.tile([P, C], F32, name="bank")
+        for piece in pieces:
+            quantise(codes0[:, piece], scales0[:, piece], early_in[:, piece, :])
+            product(first_bank[:, piece], first_words[:, :block], 0, 0, codes0[:, piece], scales0[:, piece])
+        nc.vector.tensor_copy(
+            early_in[:, GROUP - MIN_STEPPED :, 3], raws[3][:].indirect(listed(GROUP - MIN_STEPPED, GROUP))
+        )
+        early_banks = [None] + [psum.tile([P, GROUP], F32, name="bank") for t in range(1, NT)]
+        for t in (1, 2):
+            product(early_banks[t][:, :C], first_words[:, block * t : block * (t + 1)], 0, t, codes0[:], scales0[:])
+
+        first_result = tile([P, C], F32, "first_result")
+        nc.vector.tensor_tensor(first_result[:], first_bank[:], gates[:, :C], MULT)
+        codes1 = tile([P, C], U32, "codes1", "chain")
+        scales1 = tile([P, C], U8, "scales1")
+        quantise(codes1[:], scales1[:], early_in[:, C:, :])
+        nc.vector.tensor_tensor(windows[0][:].indirect(listed(0, C)), first_result[:], nothing[:], ADD)
+        windows.append(tile([P, T], F32, "window2", "early_in"))
+        nc.gpsimd.memset(windows[2][:], 0.0)
+        second_bank = psum.tile([P, C], F32, name="bank")
+        for t in (1, 2, 0, 3):
+            target = early_banks[t][:, C:] if t else second_bank[:]
+            product(target, words1[:, block * t : block * (t + 1)], 1, t, codes1[:], scales1[:])
+        product(early_banks[3][:, :C], words0[:], 0, 3, codes0[:], scales0[:])
+
+        plane = tile([P, T], BF16, "plane3")
+        planes.append(plane)
+        nc.vector.tensor_copy(plane[:, :VECTOR_ROUNDS_LAST], raws[3][:, :VECTOR_ROUNDS_LAST])
+        nc.scalar.activation(plane[:, VECTOR_ROUNDS_LAST:], raws[3][:, VECTOR_ROUNDS_LAST:], COPY)
+        nc.scalar.activation(pairs1[:, 1, :, 1], plane[:].indirect(listed(GROUP, 2 * GROUP)), COPY)
+
+        nc.sync.dma_start(gates[:, GROUP:], gate[:P, GROUP:])
+        late_words = tile([P, E - 2, 2 * N], U8, "late_words")
+        nc.sync.dma_start(
+            late_words[:].rearrange("p e b -> p (e b)").bitcast(I32).rearrange("p (e b) -> p e b", e=E - 2),
+            word_rows[:, 2:, :],
+        )
+        load_scales(2, E)
+
+        def scatter(t, first, last, values):
+            nc.vector.tensor_tensor(windows[t][:].indirect(listed(first, last)), values, gates[:, first:last], MULT)
+
+        def weave(values, pairs):
+            nc.scalar.copy(
+                values[:].rearrange("p s j -> p (s j)").bitcast(U32).rearrange("p (s h) -> p s h", h=2),
+                pairs[:].rearrange("p h s j -> p (h s j)").bitcast(U32).rearrange("p (h s) -> p s h", h=2),
+            )
+
+        def late_bank(group, t, codes, scales):
+            bank = psum.tile([P, GROUP], F32, name="bank")
+            for half in range(2):
+                e = 2 * group + half
+                cols = slice(half * C, (half + 1) * C)
+                product(bank[:, cols], late_words[:, e - 2, block * t : block * (t + 1)], e, t, codes[:, cols], scales[:, cols])
             return bank
 
-        def products(codes, scales, words, first_expert, t, result, count, copy, width=BANK):
-            for start in range(0, count, width):
-                bank = fill_bank(codes, scales, words, first_expert, t, start, width)
-                copy(result[:, start : start + width], bank[:])
+        early1 = tile([P, GROUP], F32, "early1")
+        nc.scalar.copy(early1[:], early_banks[1][:])
+        scatter(1, 0, GROUP, early1[:])
 
-        nc.vector.tensor_copy(early_in[:, :, 3], raws[3][:].indirect(early_list))
-        early_codes = held.tile([P, EARLY], U32, name="early_codes", tag="early_codes", align_bytes=64)
-        early_scales = held.tile([P, EARLY], U8, name="early_scales", align_bytes=64)
-        for e in range(early_experts):
-            cols = slice(e * C, (e + 1) * C)
-            nc.vector.quantize_mx(
-                out=early_codes[:, cols].bitcast(FP8X4),
-                scales=early_scales[:, cols],
-                in_=early_in[:, cols, :].rearrange("p w j -> p (w j)"),
-            )
-        early_results = [
-            held.tile([P, EARLY], F32, name=f"early_result{t}", tag=f"early_result{t}", align_bytes=64)
-            for t in range(NT - 1)
-        ]
-        products(early_codes, early_scales, early_words, 0, 0, early_results[0], EARLY, nc.vector.tensor_copy, C)
-        for t in range(1, NT - 1):
-            products(early_codes, early_scales, early_words, 0, t, early_results[t], EARLY, nc.scalar.copy)
-        last_bank = fill_bank(early_codes, early_scales, early_words, 0, NT - 1, 0, EARLY)
+        middle_in = tile([P, GROUP, 4], BF16, "middle_in", "chain")
+        weave(middle_in, pairs1)
+        middle_codes = tile([P, GROUP], U32, "middle_codes")
+        middle_scales = tile([P, GROUP], U8, "middle_scales")
+        quantise(middle_codes[:], middle_scales[:], middle_in[:])
+        early2 = tile([P, GROUP], F32, "early2", "pairs1")
+        nc.scalar.copy(early2[:], early_banks[2][:])
+        scatter(2, 0, GROUP, early2[:])
 
-        plane = held.tile([P, T], BF16, name="plane3", tag="early_codes", align_bytes=64)
-        nc.scalar.activation(plane[:], raws[3][:], COPY)
-        nc.scalar.activation(late_in[:, :, 3], plane[:].indirect(late_list), COPY)
-        early_results.append(held.tile([P, EARLY], F32, name="early_result3", tag="early_codes", align_bytes=64))
-        nc.scalar.copy(early_results[NT - 1][:], last_bank[:])
+        windows.append(tile([P, T], F32, "window3", "chain"))
+        nc.gpsimd.memset(windows[3][:], 0.0)
 
-        def scatter_early(t):
-            nc.vector.tensor_tensor(windows[t][:].indirect(early_list), early_results[t][:], gates[:, :EARLY], MULT)
+        middle_banks = {t: late_bank(1, t, middle_codes, middle_scales) for t in (0, 3, 1, 2)}
+        middle0 = tile([P, 2 * GROUP - C], F32, "middle0")
+        nc.scalar.copy(middle0[:, :C], second_bank[:])
+        nc.scalar.copy(middle0[:, C:], middle_banks[0][:])
+        scatter(0, C, 2 * GROUP, middle0[:])
 
-        for t in range(NT - 1):
-            scatter_early(t)
-        late_codes = held.tile([P, LATE], U32, name="late_codes", tag="early_result1", align_bytes=64)
-        late_scales = held.tile([P, LATE], U8, name="late_scales", align_bytes=64)
-        nc.vector.quantize_mx(
-            out=late_codes[:].bitcast(FP8X4),
-            scales=late_scales[:],
-            in_=late_in[:].rearrange("p w j -> p (w j)"),
-        )
-        scatter_early(NT - 1)
+        pairs2 = tile([P, 2, GROUP, 2], BF16, "pairs2", "scales1")
+        for j in range(4):
+            nc.scalar.activation(pairs2[:, j // 2, :, j % 2], planes[j][:].indirect(listed(2 * GROUP, SLOTS)), COPY)
+        last_in = tile([P, GROUP, 4], BF16, "last_in", "middle_codes")
+        weave(last_in, pairs2)
+        last_codes = tile([P, GROUP], U32, "last_codes")
+        last_scales = tile([P, GROUP], U8, "last_scales")
+        quantise(last_codes[:], last_scales[:], last_in[:])
 
-        half = T // 2
-        for t in range(NT):
-            late_result = held.tile([P, LATE], F32, name=f"late_result{t}")
-            products(late_codes, late_scales, late_words, early_experts, t, late_result, LATE, nc.scalar.copy)
-            nc.vector.tensor_tensor(windows[t][:].indirect(late_list), late_result[:], gates[:, EARLY:], MULT)
-            if t < NT - 1:
+        middle3 = tile([P, 2 * GROUP], F32, "middle3", "scales1")
+        nc.scalar.copy(middle3[:, :GROUP], early_banks[3][:])
+        nc.scalar.copy(middle3[:, GROUP:], middle_banks[3][:])
+        scatter(3, 0, 2 * GROUP, middle3[:])
+
+        for t in (0, 3):
+            bank = late_bank(2, t, last_codes, last_scales)
+            result = tile([P, GROUP], F32, f"last{t}")
+            nc.scalar.copy(result[:], bank[:])
+            scatter(t, 2 * GROUP, SLOTS, result[:])
+            nc.sync.dma_start(out[P * t : P * (t + 1), :], windows[t][:])
+        for t in (1, 2):
+            bank = late_bank(2, t, last_codes, last_scales)
+            result = tile([P, 2 * GROUP], F32, f"last{t}")
+            nc.scalar.copy(result[:, :GROUP], middle_banks[t][:])
+            nc.scalar.copy(result[:, GROUP:], bank[:])
+            scatter(t, GROUP, SLOTS, result[:])
+            if t == 1:
                 nc.sync.dma_start(out[P * t : P * (t + 1), :], windows[t][:])
             else:
-                nc.sync.dma_start(out[P * t :, :half], windows[t][:, :half])
-                nc.scalar.dma_start(out[P * t :, half:], windows[t][:, half:])
+                nc.sync.dma_start(out[P * t : P * (t + 1), :HALF], windows[t][:, :HALF])
+                nc.scalar.dma_start(out[P * t : P * (t + 1), HALF:], windows[t][:, HALF:])

@@ -20,8 +20,8 @@ NT = N // P
 ADD = mybir.AluOpType.add
 GROUP = 512
 HALF = T // 2
-VECTOR_ROUNDS = 1664
-VECTOR_ROUNDS_LAST = 384
+VECTOR_ROUNDS = 1408
+TAIL = 64
 MIN_STEPPED = T // 8
 
 
@@ -40,7 +40,7 @@ def tile_moe_pln_lin_none_kernel(tc, xT, w_words, w_scales, gate, offs, out):
             return offsets[:, first // 16 : last // 16]
 
         wplane = tile([P, E, N], U8, "wplane")
-        windows = [tile([P, T], F32, f"window{t}") for t in range(2)]
+        windows = [tile([P, T], F32, f"window{t}") for t in range(3)]
 
         nc.vector.memset(wplane[:].rearrange("p e n -> p (e n)").bitcast(I32), 0)
         zeros = windows[0][:, :HALF]
@@ -48,8 +48,8 @@ def tile_moe_pln_lin_none_kernel(tc, xT, w_words, w_scales, gate, offs, out):
         nc.scalar.activation(windows[1][:, HALF:], zeros, COPY)
         nc.vector.tensor_copy(windows[0][:, HALF:], zeros)
         nc.vector.tensor_copy(windows[1][:, :HALF], zeros)
-        nothing = tile([P, C], F32, "nothing")
-        nc.vector.memset(nothing[:].bitcast(I32), 0)
+        nc.vector.tensor_copy(windows[2][:, :HALF], zeros)
+        nc.vector.tensor_copy(windows[2][:, HALF:], zeros)
 
         x_rows = xT.rearrange("(p j) w -> p j w", j=4)
         raws = []
@@ -76,9 +76,13 @@ def tile_moe_pln_lin_none_kernel(tc, xT, w_words, w_scales, gate, offs, out):
                 )
 
         load_scales(0, 2)
-        words1 = tile([P, 2 * N], U8, "words1")
-        nc.sync.dma_start(words1[:].bitcast(I32), word_rows[:, 1, :])
+        blocks1 = word_rows[:, 1, :].rearrange("p (t b) -> p t b", t=NT)
+        inner1 = tile([P, 2, block], U8, "inner1")
+        nc.sync.dma_start(inner1[:].bitcast(I32), blocks1[:, 1:3, :])
         nc.sync.dma_start(gates[:, C:GROUP], gate[:P, C:GROUP])
+        outer1 = tile([P, 2, block], U8, "outer1")
+        nc.sync.dma_start(outer1[:].bitcast(I32), blocks1[:, 0:4:3, :])
+        words1 = [outer1[:, 0, :], inner1[:, 0, :], inner1[:, 1, :], outer1[:, 1, :]]
         words0 = tile([P, block], U8, "words0")
         nc.sync.dma_start(words0[:].bitcast(I32), word_rows[:, 0, 3 * block // 4 :])
 
@@ -131,20 +135,18 @@ def tile_moe_pln_lin_none_kernel(tc, xT, w_words, w_scales, gate, offs, out):
         codes1 = tile([P, C], U32, "codes1", "chain")
         scales1 = tile([P, C], U8, "scales1")
         quantise(codes1[:], scales1[:], early_in[:, C:, :])
-        nc.vector.tensor_tensor(windows[0][:].indirect(listed(0, C)), first_result[:], nothing[:], ADD)
-        windows.append(tile([P, T], F32, "window2", "early_in"))
-        nc.gpsimd.memset(windows[2][:], 0.0)
+        nc.vector.tensor_tensor(windows[0][:].indirect(listed(0, C)), first_result[:], windows[2][:, :C], ADD)
+        windows.append(tile([P, T], F32, "window3", "early_in"))
+        nc.gpsimd.memset(windows[3][:], 0.0)
         second_bank = psum.tile([P, C], F32, name="bank")
         for t in (1, 2, 0, 3):
             target = early_banks[t][:, C:] if t else second_bank[:]
-            product(target, words1[:, block * t : block * (t + 1)], 1, t, codes1[:], scales1[:])
+            product(target, words1[t], 1, t, codes1[:], scales1[:])
         product(early_banks[3][:, :C], words0[:], 0, 3, codes0[:], scales0[:])
 
         plane = tile([P, T], BF16, "plane3")
         planes.append(plane)
-        nc.vector.tensor_copy(plane[:, :VECTOR_ROUNDS_LAST], raws[3][:, :VECTOR_ROUNDS_LAST])
-        nc.scalar.activation(plane[:, VECTOR_ROUNDS_LAST:], raws[3][:, VECTOR_ROUNDS_LAST:], COPY)
-        nc.scalar.activation(pairs1[:, 1, :, 1], plane[:].indirect(listed(GROUP, 2 * GROUP)), COPY)
+        nc.scalar.activation(plane[:, TAIL:], raws[3][:, TAIL:], COPY)
 
         nc.sync.dma_start(gates[:, GROUP:], gate[:P, GROUP:])
         late_words = tile([P, E - 2, 2 * N], U8, "late_words")
@@ -160,7 +162,7 @@ def tile_moe_pln_lin_none_kernel(tc, xT, w_words, w_scales, gate, offs, out):
         def weave(values, pairs):
             nc.scalar.copy(
                 values[:].rearrange("p s j -> p (s j)").bitcast(U32).rearrange("p (s h) -> p s h", h=2),
-                pairs[:].rearrange("p h s j -> p (h s j)").bitcast(U32).rearrange("p (h s) -> p s h", h=2),
+                pairs.rearrange("p h s j -> p (h s j)").bitcast(U32).rearrange("p (h s) -> p s h", h=2),
             )
 
         def late_bank(group, t, codes, scales):
@@ -175,8 +177,13 @@ def tile_moe_pln_lin_none_kernel(tc, xT, w_words, w_scales, gate, offs, out):
         nc.scalar.copy(early1[:], early_banks[1][:])
         scatter(1, 0, GROUP, early1[:])
 
+        tail = tile([P, TAIL], BF16, "tail", "inner1")
+        nc.scalar.activation(tail[:], raws[3][:, :TAIL], COPY)
+        nc.scalar.activation(plane[:, :TAIL], tail[:], COPY)
+        nc.scalar.activation(pairs1[:, 1, :, 1], plane[:].indirect(listed(GROUP, 2 * GROUP)), COPY)
+
         middle_in = tile([P, GROUP, 4], BF16, "middle_in", "chain")
-        weave(middle_in, pairs1)
+        weave(middle_in, pairs1[:])
         middle_codes = tile([P, GROUP], U32, "middle_codes")
         middle_scales = tile([P, GROUP], U8, "middle_scales")
         quantise(middle_codes[:], middle_scales[:], middle_in[:])
@@ -184,30 +191,27 @@ def tile_moe_pln_lin_none_kernel(tc, xT, w_words, w_scales, gate, offs, out):
         nc.scalar.copy(early2[:], early_banks[2][:])
         scatter(2, 0, GROUP, early2[:])
 
-        windows.append(tile([P, T], F32, "window3", "chain"))
-        nc.gpsimd.memset(windows[3][:], 0.0)
-
-        middle_banks = {t: late_bank(1, t, middle_codes, middle_scales) for t in (0, 3, 1, 2)}
-        middle0 = tile([P, 2 * GROUP - C], F32, "middle0")
-        nc.scalar.copy(middle0[:, :C], second_bank[:])
-        nc.scalar.copy(middle0[:, C:], middle_banks[0][:])
-        scatter(0, C, 2 * GROUP, middle0[:])
-
-        pairs2 = tile([P, 2, GROUP, 2], BF16, "pairs2", "scales1")
-        for j in range(4):
-            nc.scalar.activation(pairs2[:, j // 2, :, j % 2], planes[j][:].indirect(listed(2 * GROUP, SLOTS)), COPY)
-        last_in = tile([P, GROUP, 4], BF16, "last_in", "middle_codes")
-        weave(last_in, pairs2)
-        last_codes = tile([P, GROUP], U32, "last_codes")
-        last_scales = tile([P, GROUP], U8, "last_scales")
-        quantise(last_codes[:], last_scales[:], last_in[:])
-
-        middle3 = tile([P, 2 * GROUP], F32, "middle3", "scales1")
+        middle_banks = {t: late_bank(1, t, middle_codes, middle_scales) for t in (3, 0, 1, 2)}
+        middle3 = tile([P, 2 * GROUP], F32, "middle3", "chain")
         nc.scalar.copy(middle3[:, :GROUP], early_banks[3][:])
         nc.scalar.copy(middle3[:, GROUP:], middle_banks[3][:])
         scatter(3, 0, 2 * GROUP, middle3[:])
 
-        for t in (0, 3):
+        pairs2 = tile([P, 2, GROUP, 2], BF16, "pairs2", "middle_scales")
+        for j in range(4):
+            nc.scalar.activation(pairs2[:, j // 2, :, j % 2], planes[j][:].indirect(listed(2 * GROUP, SLOTS)), COPY)
+        last_in = tile([P, GROUP, 4], BF16, "last_in")
+        weave(last_in, pairs2[:])
+        last_codes = tile([P, GROUP], U32, "last_codes")
+        last_scales = tile([P, GROUP], U8, "last_scales")
+        quantise(last_codes[:], last_scales[:], last_in[:])
+
+        middle0 = tile([P, 2 * GROUP - C], F32, "middle0", "middle_scales")
+        nc.scalar.copy(middle0[:, :C], second_bank[:])
+        nc.scalar.copy(middle0[:, C:], middle_banks[0][:])
+        scatter(0, C, 2 * GROUP, middle0[:])
+
+        for t in (3, 0):
             bank = late_bank(2, t, last_codes, last_scales)
             result = tile([P, GROUP], F32, f"last{t}")
             nc.scalar.copy(result[:], bank[:])
@@ -215,7 +219,7 @@ def tile_moe_pln_lin_none_kernel(tc, xT, w_words, w_scales, gate, offs, out):
             nc.sync.dma_start(out[P * t : P * (t + 1), :], windows[t][:])
         for t in (1, 2):
             bank = late_bank(2, t, last_codes, last_scales)
-            result = tile([P, 2 * GROUP], F32, f"last{t}")
+            result = tile([P, 2 * GROUP], F32, f"last{t}", "last_in" if t == 1 else "last_scales")
             nc.scalar.copy(result[:, :GROUP], middle_banks[t][:])
             nc.scalar.copy(result[:, GROUP:], bank[:])
             scatter(t, GROUP, SLOTS, result[:])

@@ -177,6 +177,10 @@ def tile_moe_pln_lin_none_kernel(tc, xT, w_words, w_scales, gate, offs, out):
         nc.scalar.copy(early1[:], early_banks[1][:])
         scatter(1, 0, GROUP, early1[:])
 
+        early2 = tile([P, GROUP], F32, "early2")
+        nc.scalar.copy(early2[:], early_banks[2][:])
+        scatter(2, 0, GROUP, early2[:])
+
         tail = tile([P, TAIL], BF16, "tail", "inner1")
         nc.scalar.activation(tail[:], raws[3][:, :TAIL], COPY)
         nc.scalar.activation(plane[:, :TAIL], tail[:], COPY)
@@ -187,43 +191,42 @@ def tile_moe_pln_lin_none_kernel(tc, xT, w_words, w_scales, gate, offs, out):
         middle_codes = tile([P, GROUP], U32, "middle_codes")
         middle_scales = tile([P, GROUP], U8, "middle_scales")
         quantise(middle_codes[:], middle_scales[:], middle_in[:])
-        early2 = tile([P, GROUP], F32, "early2", "pairs1")
-        nc.scalar.copy(early2[:], early_banks[2][:])
-        scatter(2, 0, GROUP, early2[:])
+        early3 = tile([P, GROUP], F32, "early3", "pairs1")
+        nc.scalar.copy(early3[:], early_banks[3][:])
+        scatter(3, 0, GROUP, early3[:])
 
-        middle_banks = {t: late_bank(1, t, middle_codes, middle_scales) for t in (3, 0, 1, 2)}
-        middle3 = tile([P, 2 * GROUP], F32, "middle3", "chain")
-        nc.scalar.copy(middle3[:, :GROUP], early_banks[3][:])
-        nc.scalar.copy(middle3[:, GROUP:], middle_banks[3][:])
-        scatter(3, 0, 2 * GROUP, middle3[:])
+        middle_banks = [late_bank(1, t, middle_codes, middle_scales) for t in range(NT)]
+        middle0 = tile([P, 2 * GROUP - C], F32, "middle0", "chain")
+        nc.scalar.copy(middle0[:, :C], second_bank[:])
+        nc.scalar.copy(middle0[:, C:], middle_banks[0][:])
+        scatter(0, C, 2 * GROUP, middle0[:])
 
-        pairs2 = tile([P, 2, GROUP, 2], BF16, "pairs2", "middle_scales")
+        pairs2 = tile([P, 2, GROUP, 2], BF16, "pairs2", "inner1")
         for j in range(4):
             nc.scalar.activation(pairs2[:, j // 2, :, j % 2], planes[j][:].indirect(listed(2 * GROUP, SLOTS)), COPY)
-        last_in = tile([P, GROUP, 4], BF16, "last_in")
+        last_in = tile([P, GROUP, 4], BF16, "last_in", "middle_codes")
         weave(last_in, pairs2[:])
         last_codes = tile([P, GROUP], U32, "last_codes")
         last_scales = tile([P, GROUP], U8, "last_scales")
         quantise(last_codes[:], last_scales[:], last_in[:])
 
-        middle0 = tile([P, 2 * GROUP - C], F32, "middle0", "middle_scales")
-        nc.scalar.copy(middle0[:, :C], second_bank[:])
-        nc.scalar.copy(middle0[:, C:], middle_banks[0][:])
-        scatter(0, C, 2 * GROUP, middle0[:])
+        middle1 = tile([P, GROUP], F32, "middle1", "inner1")
+        nc.scalar.copy(middle1[:], middle_banks[1][:])
+        scatter(1, GROUP, 2 * GROUP, middle1[:])
 
-        for t in (3, 0):
+        for t in (0, 1):
             bank = late_bank(2, t, last_codes, last_scales)
             result = tile([P, GROUP], F32, f"last{t}")
             nc.scalar.copy(result[:], bank[:])
             scatter(t, 2 * GROUP, SLOTS, result[:])
             nc.sync.dma_start(out[P * t : P * (t + 1), :], windows[t][:])
-        for t in (1, 2):
+        for t in (2, 3):
             bank = late_bank(2, t, last_codes, last_scales)
-            result = tile([P, 2 * GROUP], F32, f"last{t}", "last_in" if t == 1 else "last_scales")
+            result = tile([P, 2 * GROUP], F32, f"last{t}", "middle_codes" if t == 2 else "last_scales")
             nc.scalar.copy(result[:, :GROUP], middle_banks[t][:])
             nc.scalar.copy(result[:, GROUP:], bank[:])
             scatter(t, GROUP, SLOTS, result[:])
-            if t == 1:
+            if t == 2:
                 nc.sync.dma_start(out[P * t : P * (t + 1), :], windows[t][:])
             else:
                 nc.sync.dma_start(out[P * t : P * (t + 1), :HALF], windows[t][:, :HALF])

@@ -18,11 +18,13 @@ COPY = mybir.ActivationFunctionType.Copy
 
 NT = N // P
 ADD = mybir.AluOpType.add
-GROUP = 512
+EARLY = 384
+MIDDLE = 512
+LAST = SLOTS - EARLY - MIDDLE
+CUT = EARLY + MIDDLE
 HALF = T // 2
-VECTOR_ROUNDS = 1408
+VECTOR_ROUNDS = 1664
 TAIL = 64
-MIN_STEPPED = T // 8
 
 
 def tile_moe_pln_lin_none_kernel(tc, xT, w_words, w_scales, gate, offs, out):
@@ -76,26 +78,22 @@ def tile_moe_pln_lin_none_kernel(tc, xT, w_words, w_scales, gate, offs, out):
                 )
 
         load_scales(0, 2)
-        blocks1 = word_rows[:, 1, :].rearrange("p (t b) -> p t b", t=NT)
-        inner1 = tile([P, 2, block], U8, "inner1")
-        nc.sync.dma_start(inner1[:].bitcast(I32), blocks1[:, 1:3, :])
-        nc.sync.dma_start(gates[:, C:GROUP], gate[:P, C:GROUP])
-        outer1 = tile([P, 2, block], U8, "outer1")
-        nc.sync.dma_start(outer1[:].bitcast(I32), blocks1[:, 0:4:3, :])
-        words1 = [outer1[:, 0, :], inner1[:, 0, :], inner1[:, 1, :], outer1[:, 1, :]]
+        words1 = tile([P, 2 * N], U8, "words1")
+        nc.sync.dma_start(words1[:].bitcast(I32), word_rows[:, 1, :])
+        nc.sync.dma_start(gates[:, C:EARLY], gate[:P, C:EARLY])
         words0 = tile([P, block], U8, "words0")
         nc.sync.dma_start(words0[:].bitcast(I32), word_rows[:, 0, 3 * block // 4 :])
 
-        early_in = tile([P, GROUP, 4], BF16, "early_in")
-        pairs1 = tile([P, 2, GROUP, 2], BF16, "pairs1")
+        early_in = tile([P, EARLY, 4], BF16, "early_in")
+        pairs1 = tile([P, 2, MIDDLE, 2], BF16, "pairs1")
         planes = []
         for j in range(3):
             plane = tile([P, T], BF16, f"plane{j}")
             planes.append(plane)
             nc.vector.tensor_copy(plane[:, :VECTOR_ROUNDS], raws[j][:, :VECTOR_ROUNDS])
             nc.scalar.activation(plane[:, VECTOR_ROUNDS:], raws[j][:, VECTOR_ROUNDS:], COPY)
-            nc.vector.tensor_copy(early_in[:, :, j], raws[j][:].indirect(listed(0, GROUP)))
-            nc.scalar.activation(pairs1[:, j // 2, :, j % 2], plane[:].indirect(listed(GROUP, 2 * GROUP)), COPY)
+            nc.vector.tensor_copy(early_in[:, :, j], raws[j][:].indirect(listed(0, EARLY)))
+            nc.scalar.activation(pairs1[:, j // 2, :, j % 2], plane[:].indirect(listed(EARLY, CUT)), COPY)
 
         def quantise(codes, scales, values):
             nc.vector.quantize_mx(out=codes.bitcast(FP8X4), scales=scales, in_=values.rearrange("p w j -> p (w j)"))
@@ -111,7 +109,7 @@ def tile_moe_pln_lin_none_kernel(tc, xT, w_words, w_scales, gate, offs, out):
                 stop=True,
             )
 
-        pieces = [slice(P, 2 * P), slice(0, P)]
+        pieces = [slice(0, P), slice(P, 2 * P)]
         dense = [tile([P, P], BF16, f"dense{i}") for i in range(2)]
         for piece, picked in zip(pieces, dense):
             nc.vector.tensor_copy(picked[:], raws[3][:].indirect(listed(piece.start, piece.stop)))
@@ -123,32 +121,32 @@ def tile_moe_pln_lin_none_kernel(tc, xT, w_words, w_scales, gate, offs, out):
         for piece in pieces:
             quantise(codes0[:, piece], scales0[:, piece], early_in[:, piece, :])
             product(first_bank[:, piece], first_words[:, :block], 0, 0, codes0[:, piece], scales0[:, piece])
-        nc.vector.tensor_copy(
-            early_in[:, GROUP - MIN_STEPPED :, 3], raws[3][:].indirect(listed(GROUP - MIN_STEPPED, GROUP))
-        )
-        early_banks = [None] + [psum.tile([P, GROUP], F32, name="bank") for t in range(1, NT)]
+        picked = tile([P, P], BF16, "dense2", "dense1")
+        nc.vector.tensor_copy(picked[:], raws[3][:].indirect(listed(C, EARLY)))
+        nc.vector.tensor_copy(early_in[:, C:, 3], picked[:])
+        early_banks = [None] + [psum.tile([P, EARLY], F32, name="bank") for t in range(1, NT)]
         for t in (1, 2):
             product(early_banks[t][:, :C], first_words[:, block * t : block * (t + 1)], 0, t, codes0[:], scales0[:])
 
         first_result = tile([P, C], F32, "first_result")
         nc.vector.tensor_tensor(first_result[:], first_bank[:], gates[:, :C], MULT)
-        codes1 = tile([P, C], U32, "codes1", "chain")
-        scales1 = tile([P, C], U8, "scales1")
+        codes1 = tile([P, P], U32, "codes1", "chain")
+        scales1 = tile([P, P], U8, "scales1")
         quantise(codes1[:], scales1[:], early_in[:, C:, :])
         nc.vector.tensor_tensor(windows[0][:].indirect(listed(0, C)), first_result[:], windows[2][:, :C], ADD)
         windows.append(tile([P, T], F32, "window3", "early_in"))
         nc.gpsimd.memset(windows[3][:], 0.0)
-        second_bank = psum.tile([P, C], F32, name="bank")
+        second_bank = psum.tile([P, P], F32, name="bank")
         for t in (1, 2, 0, 3):
             target = early_banks[t][:, C:] if t else second_bank[:]
-            product(target, words1[t], 1, t, codes1[:], scales1[:])
+            product(target, words1[:, block * t : block * (t + 1)], 1, t, codes1[:], scales1[:])
         product(early_banks[3][:, :C], words0[:], 0, 3, codes0[:], scales0[:])
 
         plane = tile([P, T], BF16, "plane3")
         planes.append(plane)
         nc.scalar.activation(plane[:, TAIL:], raws[3][:, TAIL:], COPY)
 
-        nc.sync.dma_start(gates[:, GROUP:], gate[:P, GROUP:])
+        nc.sync.dma_start(gates[:, EARLY:], gate[:P, EARLY:])
         late_words = tile([P, E - 2, 2 * N], U8, "late_words")
         nc.sync.dma_start(
             late_words[:].rearrange("p e b -> p (e b)").bitcast(I32).rearrange("p (e b) -> p e b", e=E - 2),
@@ -165,69 +163,67 @@ def tile_moe_pln_lin_none_kernel(tc, xT, w_words, w_scales, gate, offs, out):
                 pairs.rearrange("p h s j -> p (h s j)").bitcast(U32).rearrange("p (h s) -> p s h", h=2),
             )
 
-        def late_bank(group, t, codes, scales):
-            bank = psum.tile([P, GROUP], F32, name="bank")
-            for half in range(2):
-                e = 2 * group + half
-                cols = slice(half * C, (half + 1) * C)
-                product(bank[:, cols], late_words[:, e - 2, block * t : block * (t + 1)], e, t, codes[:, cols], scales[:, cols])
+        def late_bank(first, last, start, t, codes, scales):
+            bank = psum.tile([P, last - first], F32, name="bank")
+            edges = sorted({first, last} | set(range(-(-first // C) * C, last, C)))
+            for left, right in zip(edges, edges[1:]):
+                e = left // C
+                words = words1[:] if e == 1 else late_words[:, e - 2, :]
+                cols = slice(left - start, right - start)
+                product(bank[:, left - first : right - first], words[:, block * t : block * (t + 1)], e, t, codes[:, cols], scales[:, cols])
             return bank
 
-        early1 = tile([P, GROUP], F32, "early1")
-        nc.scalar.copy(early1[:], early_banks[1][:])
-        scatter(1, 0, GROUP, early1[:])
+        for t in (1, 2):
+            result = tile([P, EARLY], F32, f"early{t}")
+            nc.scalar.copy(result[:], early_banks[t][:])
+            scatter(t, 0, EARLY, result[:])
 
-        early2 = tile([P, GROUP], F32, "early2")
-        nc.scalar.copy(early2[:], early_banks[2][:])
-        scatter(2, 0, GROUP, early2[:])
-
-        tail = tile([P, TAIL], BF16, "tail", "inner1")
+        tail = tile([P, TAIL], BF16, "tail", "scales1")
         nc.scalar.activation(tail[:], raws[3][:, :TAIL], COPY)
         nc.scalar.activation(plane[:, :TAIL], tail[:], COPY)
-        nc.scalar.activation(pairs1[:, 1, :, 1], plane[:].indirect(listed(GROUP, 2 * GROUP)), COPY)
+        nc.scalar.activation(pairs1[:, 1, :, 1], plane[:].indirect(listed(EARLY, CUT)), COPY)
 
-        middle_in = tile([P, GROUP, 4], BF16, "middle_in", "chain")
+        middle_in = tile([P, MIDDLE, 4], BF16, "middle_in", "chain")
         weave(middle_in, pairs1[:])
-        middle_codes = tile([P, GROUP], U32, "middle_codes")
-        middle_scales = tile([P, GROUP], U8, "middle_scales")
+        middle_codes = tile([P, MIDDLE], U32, "middle_codes")
+        middle_scales = tile([P, MIDDLE], U8, "middle_scales")
         quantise(middle_codes[:], middle_scales[:], middle_in[:])
-        early3 = tile([P, GROUP], F32, "early3", "pairs1")
+        early3 = tile([P, EARLY], F32, "early3", "pairs1")
         nc.scalar.copy(early3[:], early_banks[3][:])
-        scatter(3, 0, GROUP, early3[:])
+        scatter(3, 0, EARLY, early3[:])
 
-        middle_banks = [late_bank(1, t, middle_codes, middle_scales) for t in range(NT)]
-        middle0 = tile([P, 2 * GROUP - C], F32, "middle0", "chain")
-        nc.scalar.copy(middle0[:, :C], second_bank[:])
-        nc.scalar.copy(middle0[:, C:], middle_banks[0][:])
-        scatter(0, C, 2 * GROUP, middle0[:])
+        middle_banks = [late_bank(EARLY, CUT, EARLY, t, middle_codes, middle_scales) for t in range(NT)]
+        middle0 = tile([P, CUT - C], F32, "middle0", "chain")
+        nc.scalar.copy(middle0[:, : EARLY - C], second_bank[:])
+        nc.scalar.copy(middle0[:, EARLY - C :], middle_banks[0][:])
+        scatter(0, C, CUT, middle0[:])
+        for t in (1, 2):
+            result = tile([P, MIDDLE], F32, f"middle{t}")
+            nc.scalar.copy(result[:], middle_banks[t][:])
+            scatter(t, EARLY, CUT, result[:])
 
-        pairs2 = tile([P, 2, GROUP, 2], BF16, "pairs2", "inner1")
+        pairs2 = tile([P, 2, LAST, 2], BF16, "pairs2", "middle_scales")
         for j in range(4):
-            nc.scalar.activation(pairs2[:, j // 2, :, j % 2], planes[j][:].indirect(listed(2 * GROUP, SLOTS)), COPY)
-        last_in = tile([P, GROUP, 4], BF16, "last_in", "middle_codes")
+            nc.scalar.activation(pairs2[:, j // 2, :, j % 2], planes[j][:].indirect(listed(CUT, SLOTS)), COPY)
+        last_in = tile([P, LAST, 4], BF16, "last_in")
         weave(last_in, pairs2[:])
-        last_codes = tile([P, GROUP], U32, "last_codes")
-        last_scales = tile([P, GROUP], U8, "last_scales")
-        quantise(last_codes[:], last_scales[:], last_in[:])
+        last_codes = tile([P, LAST], U32, "last_codes")
+        last_scales = tile([P, LAST], U8, "last_scales")
+        for cols in (slice(0, MIDDLE), slice(MIDDLE, LAST)):
+            quantise(last_codes[:, cols], last_scales[:, cols], last_in[:, cols, :])
 
-        middle1 = tile([P, GROUP], F32, "middle1", "inner1")
-        nc.scalar.copy(middle1[:], middle_banks[1][:])
-        scatter(1, GROUP, 2 * GROUP, middle1[:])
+        middle3 = tile([P, MIDDLE], F32, "middle3", "middle_scales")
+        nc.scalar.copy(middle3[:], middle_banks[3][:])
+        scatter(3, EARLY, CUT, middle3[:])
 
-        for t in (0, 1):
-            bank = late_bank(2, t, last_codes, last_scales)
-            result = tile([P, GROUP], F32, f"last{t}")
-            nc.scalar.copy(result[:], bank[:])
-            scatter(t, 2 * GROUP, SLOTS, result[:])
-            nc.sync.dma_start(out[P * t : P * (t + 1), :], windows[t][:])
-        for t in (2, 3):
-            bank = late_bank(2, t, last_codes, last_scales)
-            result = tile([P, 2 * GROUP], F32, f"last{t}", "middle_codes" if t == 2 else "last_scales")
-            nc.scalar.copy(result[:, :GROUP], middle_banks[t][:])
-            nc.scalar.copy(result[:, GROUP:], bank[:])
-            scatter(t, GROUP, SLOTS, result[:])
-            if t == 2:
+        for t in range(NT):
+            result = tile([P, LAST], F32, f"last{t}")
+            for first, last in ((CUT, SLOTS - C), (SLOTS - C, SLOTS)):
+                bank = late_bank(first, last, CUT, t, last_codes, last_scales)
+                nc.scalar.copy(result[:, first - CUT : last - CUT], bank[:])
+            scatter(t, CUT, SLOTS, result[:])
+            if t < NT - 1:
                 nc.sync.dma_start(out[P * t : P * (t + 1), :], windows[t][:])
             else:
-                nc.sync.dma_start(out[P * t : P * (t + 1), :HALF], windows[t][:, :HALF])
-                nc.scalar.dma_start(out[P * t : P * (t + 1), HALF:], windows[t][:, HALF:])
+                nc.sync.dma_start(out[P * t :, :HALF], windows[t][:, :HALF])
+                nc.scalar.dma_start(out[P * t :, HALF:], windows[t][:, HALF:])

@@ -41,7 +41,9 @@ def tile_moe_pln_lin_none_kernel(tc, xT, w_words, w_scales, gate, offs, out):
         def listed(first, last):
             return offsets[:, first // 16 : last // 16]
 
-        wplane = tile([P, E, N], U8, "wplane")
+        first_plane = tile([P, N], U8, "first_plane")
+        nc.vector.memset(first_plane[:].bitcast(I32), 0)
+        wplane = tile([P, E - 1, N], U8, "wplane")
         windows = [tile([P, T], F32, f"window{t}") for t in range(3)]
 
         nc.vector.memset(wplane[:].rearrange("p e n -> p (e n)").bitcast(I32), 0)
@@ -53,6 +55,7 @@ def tile_moe_pln_lin_none_kernel(tc, xT, w_words, w_scales, gate, offs, out):
         nc.vector.tensor_copy(windows[2][:, :HALF], zeros)
         nc.vector.tensor_copy(windows[2][:, HALF:], zeros)
 
+        scale_rows = w_scales.bitcast(I32).rearrange("e a q n -> q (e a) n")
         x_rows = xT.rearrange("(p j) w -> p j w", j=4)
         raws = []
         for j in range(4):
@@ -61,6 +64,10 @@ def tile_moe_pln_lin_none_kernel(tc, xT, w_words, w_scales, gate, offs, out):
             raws.append(raw)
             if j == 0:
                 nc.sync.dma_start(offsets[:], offs)
+                for quad in range(4):
+                    nc.sync.dma_start(
+                        first_plane[32 * quad : 32 * quad + 4, :].bitcast(I32), scale_rows[4 * quad : 4 * quad + 4, 0]
+                    )
 
         gates = tile([P, SLOTS], F32, "gates")
         nc.sync.dma_start(gates[:, :C], gate[:P, :C])
@@ -68,16 +75,16 @@ def tile_moe_pln_lin_none_kernel(tc, xT, w_words, w_scales, gate, offs, out):
         block = 2 * P
         first_words = tile([P, 3 * block], U8, "first_words", "chain")
         nc.sync.dma_start(first_words[:].bitcast(I32), word_rows[:, 0, : 3 * block // 4])
-        plane_words = wplane[:].rearrange("p e n -> p (e n)").bitcast(I32).rearrange("p (e n) -> p e n", e=E)
-        scale_rows = w_scales.bitcast(I32).rearrange("e a q n -> q (e a) n")
+        plane_words = wplane[:].rearrange("p e n -> p (e n)").bitcast(I32).rearrange("p (e n) -> p e n", e=E - 1)
 
         def load_scales(first, last):
             for quad in range(4):
                 nc.sync.dma_start(
-                    plane_words[32 * quad : 32 * quad + 4, first:last], scale_rows[4 * quad : 4 * quad + 4, first:last]
+                    plane_words[32 * quad : 32 * quad + 4, first - 1 : last - 1],
+                    scale_rows[4 * quad : 4 * quad + 4, first:last]
                 )
 
-        load_scales(0, 2)
+        load_scales(1, 2)
         words1 = tile([P, 2 * N], U8, "words1")
         nc.sync.dma_start(words1[:].bitcast(I32), word_rows[:, 1, :])
         nc.sync.dma_start(gates[:, C:EARLY], gate[:P, C:EARLY])
@@ -102,7 +109,7 @@ def tile_moe_pln_lin_none_kernel(tc, xT, w_words, w_scales, gate, offs, out):
             nc.tensor.matmul_mx(
                 out=target,
                 lhsT=words.bitcast(FP4X4),
-                lhsT_scale=wplane[:, e, P * t : P * (t + 1)],
+                lhsT_scale=(wplane[:, e - 1, :] if e else first_plane[:])[:, P * t : P * (t + 1)],
                 rhs=codes.bitcast(FP8X4),
                 rhs_scale=scales,
                 start=True,

@@ -41,9 +41,9 @@ def tile_moe_pln_lin_none_kernel(tc, xT, w_words, w_scales, gate, offs, out):
         def listed(first, last):
             return offsets[:, first // 16 : last // 16]
 
-        first_plane = tile([P, N], U8, "first_plane")
+        first_plane = tile([P, 2, N], U8, "first_plane")
         nc.vector.memset(first_plane[:].bitcast(I32), 0)
-        wplane = tile([P, E - 1, N], U8, "wplane")
+        wplane = tile([P, E - 2, N], U8, "wplane")
         windows = [tile([P, T], F32, f"window{t}") for t in range(3)]
 
         nc.vector.memset(wplane[:].rearrange("p e n -> p (e n)").bitcast(I32), 0)
@@ -66,25 +66,24 @@ def tile_moe_pln_lin_none_kernel(tc, xT, w_words, w_scales, gate, offs, out):
                 nc.sync.dma_start(offsets[:], offs)
                 for quad in range(4):
                     nc.sync.dma_start(
-                        first_plane[32 * quad : 32 * quad + 4, :].bitcast(I32), scale_rows[4 * quad : 4 * quad + 4, 0]
+                        first_plane[32 * quad : 32 * quad + 4].bitcast(I32), scale_rows[4 * quad : 4 * quad + 4, :2]
                     )
 
         gates = tile([P, SLOTS], F32, "gates")
-        nc.sync.dma_start(gates[:, :C], gate[:P, :C])
         word_rows = w_words.bitcast(I32).rearrange("e a p b -> p (e a) b")
         block = 2 * P
         first_words = tile([P, 3 * block], U8, "first_words", "chain")
         nc.sync.dma_start(first_words[:].bitcast(I32), word_rows[:, 0, : 3 * block // 4])
-        plane_words = wplane[:].rearrange("p e n -> p (e n)").bitcast(I32).rearrange("p (e n) -> p e n", e=E - 1)
+        nc.sync.dma_start(gates[:, :C], gate[:P, :C])
+        plane_words = wplane[:].rearrange("p e n -> p (e n)").bitcast(I32).rearrange("p (e n) -> p e n", e=E - 2)
 
         def load_scales(first, last):
             for quad in range(4):
                 nc.sync.dma_start(
-                    plane_words[32 * quad : 32 * quad + 4, first - 1 : last - 1],
+                    plane_words[32 * quad : 32 * quad + 4, first - 2 : last - 2],
                     scale_rows[4 * quad : 4 * quad + 4, first:last]
                 )
 
-        load_scales(1, 2)
         words1 = tile([P, 2 * N], U8, "words1")
         nc.sync.dma_start(words1[:].bitcast(I32), word_rows[:, 1, :])
         nc.sync.dma_start(gates[:, C:EARLY], gate[:P, C:EARLY])
@@ -109,7 +108,7 @@ def tile_moe_pln_lin_none_kernel(tc, xT, w_words, w_scales, gate, offs, out):
             nc.tensor.matmul_mx(
                 out=target,
                 lhsT=words.bitcast(FP4X4),
-                lhsT_scale=(wplane[:, e - 1, :] if e else first_plane[:])[:, P * t : P * (t + 1)],
+                lhsT_scale=(wplane[:, e - 2, :] if e > 1 else first_plane[:, e, :])[:, P * t : P * (t + 1)],
                 rhs=codes.bitcast(FP8X4),
                 rhs_scale=scales,
                 start=True,
@@ -144,8 +143,9 @@ def tile_moe_pln_lin_none_kernel(tc, xT, w_words, w_scales, gate, offs, out):
         windows.append(tile([P, T], F32, "window3", "early_in"))
         nc.gpsimd.memset(windows[3][:], 0.0)
         second_bank = psum.tile([P, P], F32, name="bank")
+        third_bank = psum.tile([P, P], F32, name="bank")
         for t in (1, 2, 0, 3):
-            target = early_banks[t][:, C:] if t else second_bank[:]
+            target = early_banks[t][:, C:] if t > 1 else (second_bank, third_bank)[t][:]
             product(target, words1[:, block * t : block * (t + 1)], 1, t, codes1[:], scales1[:])
         product(early_banks[3][:, :C], words0[:], 0, 3, codes0[:], scales0[:])
 
@@ -182,7 +182,11 @@ def tile_moe_pln_lin_none_kernel(tc, xT, w_words, w_scales, gate, offs, out):
 
         for t in (1, 2):
             result = tile([P, EARLY], F32, f"early{t}")
-            nc.scalar.copy(result[:], early_banks[t][:])
+            if t == 1:
+                nc.scalar.copy(result[:, :C], early_banks[t][:, :C])
+                nc.scalar.copy(result[:, C:], third_bank[:])
+            else:
+                nc.scalar.copy(result[:], early_banks[t][:])
             scatter(t, 0, EARLY, result[:])
 
         tail = tile([P, TAIL], BF16, "tail", "scales1")

@@ -44,7 +44,7 @@ def tile_moe_pln_lin_none_kernel(tc, xT, w_words, w_scales, gate, offs, out):
         first_plane = tile([P, 2, N], U8, "first_plane")
         nc.vector.memset(first_plane[:].bitcast(I32), 0)
         wplane = tile([P, E - 2, N], U8, "wplane")
-        windows = [tile([P, T], F32, f"window{t}") for t in range(3)]
+        windows = [tile([P, T], F32, f"window{t}") for t in range(NT)]
 
         nc.vector.memset(wplane[:].rearrange("p e n -> p (e n)").bitcast(I32), 0)
         zeros = windows[0][:, :HALF]
@@ -54,6 +54,8 @@ def tile_moe_pln_lin_none_kernel(tc, xT, w_words, w_scales, gate, offs, out):
         nc.vector.tensor_copy(windows[1][:, :HALF], zeros)
         nc.vector.tensor_copy(windows[2][:, :HALF], zeros)
         nc.vector.tensor_copy(windows[2][:, HALF:], zeros)
+        nc.vector.tensor_copy(windows[3][:, :HALF], zeros)
+        nc.scalar.activation(windows[3][:, HALF:], zeros, COPY)
 
         scale_rows = w_scales.bitcast(I32).rearrange("e a q n -> q (e a) n")
         x_rows = xT.rearrange("(p j) w -> p j w", j=4)
@@ -72,8 +74,8 @@ def tile_moe_pln_lin_none_kernel(tc, xT, w_words, w_scales, gate, offs, out):
         gates = tile([P, SLOTS], F32, "gates")
         word_rows = w_words.bitcast(I32).rearrange("e a p b -> p (e a) b")
         block = 2 * P
-        first_words = tile([P, 3 * block], U8, "first_words", "chain")
-        nc.sync.dma_start(first_words[:].bitcast(I32), word_rows[:, 0, : 3 * block // 4])
+        first_words = tile([P, 1 * block], U8, "first_words", "chain")
+        nc.sync.dma_start(first_words[:].bitcast(I32), word_rows[:, 0, : 1 * block // 4])
         nc.sync.dma_start(gates[:, :C], gate[:P, :C])
         plane_words = wplane[:].rearrange("p e n -> p (e n)").bitcast(I32).rearrange("p (e n) -> p e n", e=E - 2)
 
@@ -84,11 +86,13 @@ def tile_moe_pln_lin_none_kernel(tc, xT, w_words, w_scales, gate, offs, out):
                     scale_rows[4 * quad : 4 * quad + 4, first:last]
                 )
 
+        words0 = tile([P, 3 * block], U8, "words0")
+        nc.sync.dma_start(words0[:].bitcast(I32), word_rows[:, 0, 1 * block // 4 :])
+        blocks0 = [first_words[:, block * t : block * (t + 1)] for t in range(1)]
+        blocks0 = blocks0 + [words0[:, block * t : block * (t + 1)] for t in range(3)]
         words1 = tile([P, 2 * N], U8, "words1")
         nc.sync.dma_start(words1[:].bitcast(I32), word_rows[:, 1, :])
         nc.sync.dma_start(gates[:, C:EARLY], gate[:P, C:EARLY])
-        words0 = tile([P, block], U8, "words0")
-        nc.sync.dma_start(words0[:].bitcast(I32), word_rows[:, 0, 3 * block // 4 :])
 
         early_in = tile([P, EARLY, 4], BF16, "early_in")
         pairs1 = tile([P, 2, MIDDLE, 2], BF16, "pairs1")
@@ -126,13 +130,13 @@ def tile_moe_pln_lin_none_kernel(tc, xT, w_words, w_scales, gate, offs, out):
         first_bank = psum.tile([P, C], F32, name="bank")
         for piece in pieces:
             quantise(codes0[:, piece], scales0[:, piece], early_in[:, piece, :])
-            product(first_bank[:, piece], first_words[:, :block], 0, 0, codes0[:, piece], scales0[:, piece])
+            product(first_bank[:, piece], blocks0[0], 0, 0, codes0[:, piece], scales0[:, piece])
         picked = tile([P, P], BF16, "dense2", "dense1")
         nc.vector.tensor_copy(picked[:], raws[3][:].indirect(listed(C, EARLY)))
         nc.vector.tensor_copy(early_in[:, C:, 3], picked[:])
         early_banks = [None] + [psum.tile([P, EARLY], F32, name="bank") for t in range(1, NT)]
         for t in (1, 2):
-            product(early_banks[t][:, :C], first_words[:, block * t : block * (t + 1)], 0, t, codes0[:], scales0[:])
+            product(early_banks[t][:, :C], blocks0[t], 0, t, codes0[:], scales0[:])
 
         first_result = tile([P, C], F32, "first_result")
         nc.vector.tensor_tensor(first_result[:], first_bank[:], gates[:, :C], MULT)
@@ -140,14 +144,12 @@ def tile_moe_pln_lin_none_kernel(tc, xT, w_words, w_scales, gate, offs, out):
         scales1 = tile([P, P], U8, "scales1")
         quantise(codes1[:], scales1[:], early_in[:, C:, :])
         nc.vector.tensor_tensor(windows[0][:].indirect(listed(0, C)), first_result[:], windows[2][:, :C], ADD)
-        windows.append(tile([P, T], F32, "window3", "early_in"))
-        nc.gpsimd.memset(windows[3][:], 0.0)
         second_bank = psum.tile([P, P], F32, name="bank")
         third_bank = psum.tile([P, P], F32, name="bank")
         for t in (1, 2, 0, 3):
             target = early_banks[t][:, C:] if t > 1 else (second_bank, third_bank)[t][:]
             product(target, words1[:, block * t : block * (t + 1)], 1, t, codes1[:], scales1[:])
-        product(early_banks[3][:, :C], words0[:], 0, 3, codes0[:], scales0[:])
+        product(early_banks[3][:, :C], blocks0[3], 0, 3, codes0[:], scales0[:])
 
         plane = tile([P, T], BF16, "plane3")
         planes.append(plane)

@@ -14,17 +14,13 @@ U8 = mybir.dt.uint8
 FP8X4 = mybir.dt.float8_e4m3fn_x4
 FP4X4 = mybir.dt.float4_e2m1fn_x4
 MULT = mybir.AluOpType.mult
+ADD = mybir.AluOpType.add
 COPY = mybir.ActivationFunctionType.Copy
 
 NT = N // P
-ADD = mybir.AluOpType.add
-EARLY = 384
-MIDDLE = 512
-LAST = SLOTS - EARLY - MIDDLE
-CUT = EARLY + MIDDLE
+GROUP = 2 * C
 HALF = T // 2
-VECTOR_ROUNDS = 1664
-TAIL = 64
+BLOCK = 2 * P
 
 
 def tile_moe_pln_lin_none_kernel(tc, xT, w_words, w_scales, gate, offs, out):
@@ -73,45 +69,36 @@ def tile_moe_pln_lin_none_kernel(tc, xT, w_words, w_scales, gate, offs, out):
 
         gates = tile([P, SLOTS], F32, "gates")
         word_rows = w_words.bitcast(I32).rearrange("e a p b -> p (e a) b")
-        block = 2 * P
-        first_words = tile([P, 1 * block], U8, "first_words", "chain")
-        nc.sync.dma_start(first_words[:].bitcast(I32), word_rows[:, 0, : 1 * block // 4])
+        first_words = tile([P, BLOCK], U8, "first_words")
+        nc.sync.dma_start(first_words[:].bitcast(I32), word_rows[:, 0, : BLOCK // 4])
         nc.sync.dma_start(gates[:, :C], gate[:P, :C])
-        plane_words = wplane[:].rearrange("p e n -> p (e n)").bitcast(I32).rearrange("p (e n) -> p e n", e=E - 2)
-
-        def load_scales(first, last):
-            for quad in range(4):
-                nc.sync.dma_start(
-                    plane_words[32 * quad : 32 * quad + 4, first - 2 : last - 2],
-                    scale_rows[4 * quad : 4 * quad + 4, first:last]
-                )
-
-        words0 = tile([P, 3 * block], U8, "words0")
-        nc.sync.dma_start(words0[:].bitcast(I32), word_rows[:, 0, 1 * block // 4 :])
-        blocks0 = [first_words[:, block * t : block * (t + 1)] for t in range(1)]
-        blocks0 = blocks0 + [words0[:, block * t : block * (t + 1)] for t in range(3)]
+        words0 = tile([P, 3 * BLOCK], U8, "words0")
+        nc.sync.dma_start(words0[:].bitcast(I32), word_rows[:, 0, BLOCK // 4 :])
         words1 = tile([P, 2 * N], U8, "words1")
         nc.sync.dma_start(words1[:].bitcast(I32), word_rows[:, 1, :])
-        nc.sync.dma_start(gates[:, C:EARLY], gate[:P, C:EARLY])
+        nc.sync.dma_start(gates[:, C:GROUP], gate[:P, C:GROUP])
+        late_words = tile([P, E - 2, 2 * N], U8, "late_words")
+        nc.sync.dma_start(
+            late_words[:].rearrange("p e b -> p (e b)").bitcast(I32).rearrange("p (e b) -> p e b", e=E - 2),
+            word_rows[:, 2:, :],
+        )
+        nc.sync.dma_start(gates[:, GROUP:], gate[:P, GROUP:])
+        plane_words = wplane[:].rearrange("p e n -> p (e n)").bitcast(I32).rearrange("p (e n) -> p e n", e=E - 2)
+        for quad in range(4):
+            nc.sync.dma_start(plane_words[32 * quad : 32 * quad + 4], scale_rows[4 * quad : 4 * quad + 4, 2:])
 
-        early_in = tile([P, EARLY, 4], BF16, "early_in")
-        pairs1 = tile([P, 2, MIDDLE, 2], BF16, "pairs1")
-        planes = []
-        for j in range(3):
-            plane = tile([P, T], BF16, f"plane{j}")
-            planes.append(plane)
-            nc.vector.tensor_copy(plane[:, :VECTOR_ROUNDS], raws[j][:, :VECTOR_ROUNDS])
-            nc.scalar.activation(plane[:, VECTOR_ROUNDS:], raws[j][:, VECTOR_ROUNDS:], COPY)
-            nc.vector.tensor_copy(early_in[:, :, j], raws[j][:].indirect(listed(0, EARLY)))
-            nc.scalar.activation(pairs1[:, j // 2, :, j % 2], plane[:].indirect(listed(EARLY, CUT)), COPY)
+        def weights(e, t):
+            if e == 0:
+                return first_words[:] if t == 0 else words0[:, BLOCK * (t - 1) : BLOCK * t]
+            return (words1[:] if e == 1 else late_words[:, e - 2, :])[:, BLOCK * t : BLOCK * (t + 1)]
 
         def quantise(codes, scales, values):
             nc.vector.quantize_mx(out=codes.bitcast(FP8X4), scales=scales, in_=values.rearrange("p w j -> p (w j)"))
 
-        def product(target, words, e, t, codes, scales):
+        def product(target, e, t, codes, scales):
             nc.tensor.matmul_mx(
                 out=target,
-                lhsT=words.bitcast(FP4X4),
+                lhsT=weights(e, t).bitcast(FP4X4),
                 lhsT_scale=(wplane[:, e - 2, :] if e > 1 else first_plane[:, e, :])[:, P * t : P * (t + 1)],
                 rhs=codes.bitcast(FP8X4),
                 rhs_scale=scales,
@@ -119,122 +106,112 @@ def tile_moe_pln_lin_none_kernel(tc, xT, w_words, w_scales, gate, offs, out):
                 stop=True,
             )
 
+        def pick(target, j, first, last):
+            nc.scalar.activation(target, raws[j][:].indirect(listed(first, last)), COPY)
+
+        def scatter(t, first, last, values):
+            nc.vector.tensor_tensor(windows[t][:].indirect(listed(first, last)), values, gates[:, first:last], MULT)
+
+        def weave(values, planes):
+            nc.scalar.copy(values, planes.rearrange("p j s -> p s j"))
+
+        in0 = tile([P, C, 4], BF16, "in0")
+        in1 = tile([P, C, 4], BF16, "in1")
+        in2 = tile([P, GROUP, 4], BF16, "in2")
+        low = tile([P, 2, C + GROUP], BF16, "low")
+        planes1 = tile([P, 2, C], BF16, "planes1")
+        for j in range(3):
+            picked = tile([P, C], BF16, f"picked{j}")
+            nc.vector.tensor_copy(picked[:], raws[j][:].indirect(listed(0, C)))
+            nc.vector.tensor_copy(in0[:, :, j], picked[:])
+            if j < 2:
+                pick(low[:, j, :], j, C, 2 * GROUP)
+                nc.vector.tensor_copy(in1[:, :, j], low[:, j, :C])
+                nc.vector.tensor_copy(in2[:, :, j], low[:, j, C:])
+            else:
+                pick(planes1[:, 0, :], j, C, GROUP)
+
         pieces = [slice(0, P), slice(P, 2 * P)]
         dense = [tile([P, P], BF16, f"dense{i}") for i in range(2)]
         for piece, picked in zip(pieces, dense):
             nc.vector.tensor_copy(picked[:], raws[3][:].indirect(listed(piece.start, piece.stop)))
         for piece, picked in zip(pieces, dense):
-            nc.vector.tensor_copy(early_in[:, piece, 3], picked[:])
+            nc.vector.tensor_copy(in0[:, piece, 3], picked[:])
+        for piece in pieces:
+            pick(planes1[:, 1, piece], 3, C + piece.start, C + piece.stop)
+        for piece in pieces:
+            weave(in1[:, piece, 2:], planes1[:, :, piece])
         codes0 = tile([P, C], U32, "codes0")
         scales0 = tile([P, C], U8, "scales0")
-        first_bank = psum.tile([P, C], F32, name="bank")
+        quantise(codes0[:, :P], scales0[:, :P], in0[:, :P, :])
+        first_banks = [psum.tile([P, P], F32, name="bank") for t in range(2)]
+        for t in range(2):
+            product(first_banks[t][:], 0, t, codes0[:, :P], scales0[:, :P])
+        quantise(codes0[:, P:], scales0[:, P:], in0[:, P:, :])
+        codes1 = tile([P, C], U32, "codes1", "chain")
+        scales1 = tile([P, C], U8, "scales1")
         for piece in pieces:
-            quantise(codes0[:, piece], scales0[:, piece], early_in[:, piece, :])
-            product(first_bank[:, piece], blocks0[0], 0, 0, codes0[:, piece], scales0[:, piece])
-        picked = tile([P, P], BF16, "dense2", "dense1")
-        nc.vector.tensor_copy(picked[:], raws[3][:].indirect(listed(C, EARLY)))
-        nc.vector.tensor_copy(early_in[:, C:, 3], picked[:])
-        early_banks = [None] + [psum.tile([P, EARLY], F32, name="bank") for t in range(1, NT)]
-        for t in (1, 2):
-            product(early_banks[t][:, :C], blocks0[t], 0, t, codes0[:], scales0[:])
+            quantise(codes1[:, piece], scales1[:, piece], in1[:, piece, :])
+        firsts = [tile([P, P], F32, f"first{t}") for t in range(2)]
+        for t in range(2):
+            nc.vector.tensor_tensor(firsts[t][:], first_banks[t][:], gates[:, :P], MULT)
+        for t in range(2):
+            nc.vector.tensor_tensor(windows[t][:].indirect(listed(0, P)), firsts[t][:], windows[3][:, :P], ADD)
 
-        first_result = tile([P, C], F32, "first_result")
-        nc.vector.tensor_tensor(first_result[:], first_bank[:], gates[:, :C], MULT)
-        codes1 = tile([P, P], U32, "codes1", "chain")
-        scales1 = tile([P, P], U8, "scales1")
-        quantise(codes1[:], scales1[:], early_in[:, C:, :])
-        nc.vector.tensor_tensor(windows[0][:].indirect(listed(0, C)), first_result[:], windows[2][:, :C], ADD)
-        second_bank = psum.tile([P, P], F32, name="bank")
-        third_bank = psum.tile([P, P], F32, name="bank")
-        for t in (1, 2, 0, 3):
-            target = early_banks[t][:, C:] if t > 1 else (second_bank, third_bank)[t][:]
-            product(target, words1[:, block * t : block * (t + 1)], 1, t, codes1[:], scales1[:])
-        product(early_banks[3][:, :C], blocks0[3], 0, 3, codes0[:], scales0[:])
+        early_banks = [psum.tile([P, GROUP], F32, name="bank") for t in range(NT)]
+        product(early_banks[2][:, :C], 0, 2, codes0[:], scales0[:])
+        product(early_banks[2][:, C:], 1, 2, codes1[:], scales1[:])
+        for t in (0, 1, 3):
+            first = 0 if t == 3 else P
+            product(early_banks[t][:, C:], 1, t, codes1[:], scales1[:])
+            product(early_banks[t][:, first:C], 0, t, codes0[:, first:], scales0[:, first:])
 
-        plane = tile([P, T], BF16, "plane3")
-        planes.append(plane)
-        nc.scalar.activation(plane[:, TAIL:], raws[3][:, TAIL:], COPY)
+        for t in (2, 0, 1):
+            first = 0 if t == 2 else P
+            result = tile([P, GROUP - first], F32, f"early{t}")
+            nc.scalar.copy(result[:], early_banks[t][:, first:])
+            scatter(t, first, GROUP, result[:])
+        planes2 = tile([P, 2, GROUP], BF16, "planes2", "chain")
+        for j in (2, 3):
+            pick(planes2[:, j - 2, :], j, GROUP, 2 * GROUP)
 
-        nc.sync.dma_start(gates[:, EARLY:], gate[:P, EARLY:])
-        late_words = tile([P, E - 2, 2 * N], U8, "late_words")
-        nc.sync.dma_start(
-            late_words[:].rearrange("p e b -> p (e b)").bitcast(I32).rearrange("p (e b) -> p e b", e=E - 2),
-            word_rows[:, 2:, :],
-        )
-        load_scales(2, E)
-
-        def scatter(t, first, last, values):
-            nc.vector.tensor_tensor(windows[t][:].indirect(listed(first, last)), values, gates[:, first:last], MULT)
-
-        def weave(values, pairs):
-            nc.scalar.copy(
-                values[:].rearrange("p s j -> p (s j)").bitcast(U32).rearrange("p (s h) -> p s h", h=2),
-                pairs.rearrange("p h s j -> p (h s j)").bitcast(U32).rearrange("p (h s) -> p s h", h=2),
-            )
-
-        def late_bank(first, last, start, t, codes, scales):
-            bank = psum.tile([P, last - first], F32, name="bank")
-            edges = sorted({first, last} | set(range(-(-first // C) * C, last, C)))
-            for left, right in zip(edges, edges[1:]):
-                e = left // C
-                words = words1[:] if e == 1 else late_words[:, e - 2, :]
-                cols = slice(left - start, right - start)
-                product(bank[:, left - first : right - first], words[:, block * t : block * (t + 1)], e, t, codes[:, cols], scales[:, cols])
+        def group_bank(e, t, codes, scales):
+            bank = psum.tile([P, GROUP], F32, name="bank")
+            for half in range(2):
+                cols = slice(C * half, C * (half + 1))
+                product(bank[:, cols], e + half, t, codes[:, cols], scales[:, cols])
             return bank
 
-        for t in (1, 2):
-            result = tile([P, EARLY], F32, f"early{t}")
-            if t == 1:
-                nc.scalar.copy(result[:, :C], early_banks[t][:, :C])
-                nc.scalar.copy(result[:, C:], third_bank[:])
-            else:
-                nc.scalar.copy(result[:], early_banks[t][:])
-            scatter(t, 0, EARLY, result[:])
-
-        tail = tile([P, TAIL], BF16, "tail", "scales1")
-        nc.scalar.activation(tail[:], raws[3][:, :TAIL], COPY)
-        nc.scalar.activation(plane[:, :TAIL], tail[:], COPY)
-        nc.scalar.activation(pairs1[:, 1, :, 1], plane[:].indirect(listed(EARLY, CUT)), COPY)
-
-        middle_in = tile([P, MIDDLE, 4], BF16, "middle_in", "chain")
-        weave(middle_in, pairs1[:])
-        middle_codes = tile([P, MIDDLE], U32, "middle_codes")
-        middle_scales = tile([P, MIDDLE], U8, "middle_scales")
-        quantise(middle_codes[:], middle_scales[:], middle_in[:])
-        early3 = tile([P, EARLY], F32, "early3", "pairs1")
+        weave(in2[:, :, 2:], planes2[:])
+        codes2 = tile([P, GROUP], U32, "codes2")
+        scales2 = tile([P, GROUP], U8, "scales2")
+        quantise(codes2[:], scales2[:], in2[:])
+        early3 = tile([P, GROUP], F32, "early3", "chain")
         nc.scalar.copy(early3[:], early_banks[3][:])
-        scatter(3, 0, EARLY, early3[:])
+        scatter(3, 0, GROUP, early3[:])
 
-        middle_banks = [late_bank(EARLY, CUT, EARLY, t, middle_codes, middle_scales) for t in range(NT)]
-        middle0 = tile([P, CUT - C], F32, "middle0", "chain")
-        nc.scalar.copy(middle0[:, : EARLY - C], second_bank[:])
-        nc.scalar.copy(middle0[:, EARLY - C :], middle_banks[0][:])
-        scatter(0, C, CUT, middle0[:])
-        for t in (1, 2):
-            result = tile([P, MIDDLE], F32, f"middle{t}")
+        middle_banks = [group_bank(2, t, codes2, scales2) for t in range(NT)]
+        for t in range(3):
+            result = tile([P, GROUP], F32, f"middle{t}")
             nc.scalar.copy(result[:], middle_banks[t][:])
-            scatter(t, EARLY, CUT, result[:])
+            scatter(t, GROUP, 2 * GROUP, result[:])
 
-        pairs2 = tile([P, 2, LAST, 2], BF16, "pairs2", "middle_scales")
+        planes3 = tile([P, 4, GROUP], BF16, "planes3", "scales2")
         for j in range(4):
-            nc.scalar.activation(pairs2[:, j // 2, :, j % 2], planes[j][:].indirect(listed(CUT, SLOTS)), COPY)
-        last_in = tile([P, LAST, 4], BF16, "last_in")
-        weave(last_in, pairs2[:])
-        last_codes = tile([P, LAST], U32, "last_codes")
-        last_scales = tile([P, LAST], U8, "last_scales")
-        for cols in (slice(0, MIDDLE), slice(MIDDLE, LAST)):
-            quantise(last_codes[:, cols], last_scales[:, cols], last_in[:, cols, :])
-
-        middle3 = tile([P, MIDDLE], F32, "middle3", "middle_scales")
+            pick(planes3[:, j, :], j, 2 * GROUP, SLOTS)
+        in3 = tile([P, GROUP, 4], BF16, "in3")
+        weave(in3[:], planes3[:])
+        codes3 = tile([P, GROUP], U32, "codes3")
+        scales3 = tile([P, GROUP], U8, "scales3")
+        quantise(codes3[:], scales3[:], in3[:])
+        middle3 = tile([P, GROUP], F32, "middle3", "scales2")
         nc.scalar.copy(middle3[:], middle_banks[3][:])
-        scatter(3, EARLY, CUT, middle3[:])
+        scatter(3, GROUP, 2 * GROUP, middle3[:])
 
         for t in range(NT):
-            result = tile([P, LAST], F32, f"last{t}")
-            for first, last in ((CUT, SLOTS - C), (SLOTS - C, SLOTS)):
-                bank = late_bank(first, last, CUT, t, last_codes, last_scales)
-                nc.scalar.copy(result[:, first - CUT : last - CUT], bank[:])
-            scatter(t, CUT, SLOTS, result[:])
+            result = tile([P, GROUP], F32, f"last{t}")
+            nc.scalar.copy(result[:], group_bank(4, t, codes3, scales3)[:])
+            scatter(t, 2 * GROUP, SLOTS, result[:])
             if t < NT - 1:
                 nc.sync.dma_start(out[P * t : P * (t + 1), :], windows[t][:])
             else:

@@ -144,9 +144,9 @@ def tile_moe_pln_lin_none_kernel(tc, xT, w_words, w_scales, gate, offs, out):
         codes0 = tile([P, C], U32, "codes0")
         scales0 = tile([P, C], U8, "scales0")
         quantise(codes0[:, :P], scales0[:, :P], in0[:, :P, :])
-        first_banks = [psum.tile([P, P], F32, name="bank") for t in range(2)]
+        first_bank = psum.tile([P, 2, P], F32, name="bank")
         for t in range(2):
-            product(first_banks[t][:], 0, t, codes0[:, :P], scales0[:, :P])
+            product(first_bank[:, t, :], 0, t, codes0[:, :P], scales0[:, :P])
         quantise(codes0[:, P:], scales0[:, P:], in0[:, P:, :])
         codes1 = tile([P, C], U32, "codes1", "chain")
         scales1 = tile([P, C], U8, "scales1")
@@ -154,7 +154,7 @@ def tile_moe_pln_lin_none_kernel(tc, xT, w_words, w_scales, gate, offs, out):
             quantise(codes1[:, piece], scales1[:, piece], in1[:, piece, :])
         firsts = [tile([P, P], F32, f"first{t}") for t in range(2)]
         for t in range(2):
-            nc.vector.tensor_tensor(firsts[t][:], first_banks[t][:], gates[:, :P], MULT)
+            nc.vector.tensor_tensor(firsts[t][:], first_bank[:, t, :], gates[:, :P], MULT)
         for t in range(2):
             nc.vector.tensor_tensor(windows[t][:].indirect(listed(0, P)), firsts[t][:], windows[3][:, :P], ADD)
 
@@ -190,30 +190,37 @@ def tile_moe_pln_lin_none_kernel(tc, xT, w_words, w_scales, gate, offs, out):
         nc.scalar.copy(early3[:], early_banks[3][:])
         scatter(3, 0, GROUP, early3[:])
 
+        planes3 = tile([P, 2, GROUP], BF16, "planes3", "codes0")
+        for j in range(2):
+            pick(planes3[:, j, :], j, 2 * GROUP, SLOTS)
+
         middle_banks = [group_bank(2, t, codes2, scales2) for t in range(NT)]
-        for t in range(3):
+        for t in range(2):
             result = tile([P, GROUP], F32, f"middle{t}")
             nc.scalar.copy(result[:], middle_banks[t][:])
             scatter(t, GROUP, 2 * GROUP, result[:])
+        both = tile([P, 2 * GROUP], F32, "both")
+        nc.scalar.copy(both[:, :GROUP], middle_banks[3][:])
 
-        planes3 = tile([P, 4, GROUP], BF16, "planes3", "scales2")
-        for j in range(4):
-            pick(planes3[:, j, :], j, 2 * GROUP, SLOTS)
+        high3 = tile([P, 2, GROUP], BF16, "high3", "scales2")
+        for j in (2, 3):
+            pick(high3[:, j - 2, :], j, 2 * GROUP, SLOTS)
         in3 = tile([P, GROUP, 4], BF16, "in3")
-        weave(in3[:], planes3[:])
+        weave(in3[:, :, :2], planes3[:])
+        weave(in3[:, :, 2:], high3[:])
         codes3 = tile([P, GROUP], U32, "codes3")
         scales3 = tile([P, GROUP], U8, "scales3")
         quantise(codes3[:], scales3[:], in3[:])
-        middle3 = tile([P, GROUP], F32, "middle3", "scales2")
-        nc.scalar.copy(middle3[:], middle_banks[3][:])
-        scatter(3, GROUP, 2 * GROUP, middle3[:])
+        middle2 = tile([P, GROUP], F32, "middle2", "scales2")
+        nc.scalar.copy(middle2[:], middle_banks[2][:])
+        scatter(2, GROUP, 2 * GROUP, middle2[:])
 
-        for t in range(NT):
+        for t in range(NT - 1):
             result = tile([P, GROUP], F32, f"last{t}")
             nc.scalar.copy(result[:], group_bank(4, t, codes3, scales3)[:])
             scatter(t, 2 * GROUP, SLOTS, result[:])
-            if t < NT - 1:
-                nc.sync.dma_start(out[P * t : P * (t + 1), :], windows[t][:])
-            else:
-                nc.sync.dma_start(out[P * t :, :HALF], windows[t][:, :HALF])
-                nc.scalar.dma_start(out[P * t :, HALF:], windows[t][:, HALF:])
+            nc.sync.dma_start(out[P * t : P * (t + 1), :], windows[t][:])
+        nc.scalar.copy(both[:, GROUP:], group_bank(4, 3, codes3, scales3)[:])
+        scatter(3, GROUP, SLOTS, both[:])
+        nc.sync.dma_start(out[3 * P :, :HALF], windows[3][:, :HALF])
+        nc.scalar.dma_start(out[3 * P :, HALF:], windows[3][:, HALF:])

@@ -69,11 +69,11 @@ def tile_moe_pln_lin_none_kernel(tc, xT, w_words, w_scales, gate, offs, out):
 
         gates = tile([P, SLOTS], F32, "gates")
         word_rows = w_words.bitcast(I32).rearrange("e a p b -> p (e a) b")
-        first_words = tile([P, BLOCK], U8, "first_words")
-        nc.sync.dma_start(first_words[:].bitcast(I32), word_rows[:, 0, : BLOCK // 4])
+        first_words = tile([P, 2 * BLOCK], U8, "first_words")
+        nc.sync.dma_start(first_words[:].bitcast(I32), word_rows[:, 0, : BLOCK // 2])
         nc.sync.dma_start(gates[:, :C], gate[:P, :C])
-        words0 = tile([P, 3 * BLOCK], U8, "words0")
-        nc.sync.dma_start(words0[:].bitcast(I32), word_rows[:, 0, BLOCK // 4 :])
+        words0 = tile([P, 2 * BLOCK], U8, "words0")
+        nc.sync.dma_start(words0[:].bitcast(I32), word_rows[:, 0, BLOCK // 2 :])
         words1 = tile([P, 2 * N], U8, "words1")
         nc.sync.dma_start(words1[:].bitcast(I32), word_rows[:, 1, :])
         nc.sync.dma_start(gates[:, C:GROUP], gate[:P, C:GROUP])
@@ -89,7 +89,7 @@ def tile_moe_pln_lin_none_kernel(tc, xT, w_words, w_scales, gate, offs, out):
 
         def weights(e, t):
             if e == 0:
-                return first_words[:] if t == 0 else words0[:, BLOCK * (t - 1) : BLOCK * t]
+                return (first_words, words0)[t // 2][:, BLOCK * (t % 2) : BLOCK * (t % 2 + 1)]
             return (words1[:] if e == 1 else late_words[:, e - 2, :])[:, BLOCK * t : BLOCK * (t + 1)]
 
         def quantise(codes, scales, values):

@@ -144,30 +144,34 @@ def tile_moe_pln_lin_none_kernel(tc, xT, w_words, w_scales, gate, offs, out):
         codes0 = tile([P, C], U32, "codes0")
         scales0 = tile([P, C], U8, "scales0")
         quantise(codes0[:, :P], scales0[:, :P], in0[:, :P, :])
-        first_bank = psum.tile([P, 2, P], F32, name="bank")
-        for t in range(2):
-            product(first_bank[:, t, :], 0, t, codes0[:, :P], scales0[:, :P])
+        first_bank = psum.tile([P, P], F32, name="bank")
+        product(first_bank[:], 0, 0, codes0[:, :P], scales0[:, :P])
         quantise(codes0[:, P:], scales0[:, P:], in0[:, P:, :])
         codes1 = tile([P, C], U32, "codes1", "chain")
         scales1 = tile([P, C], U8, "scales1")
         for piece in pieces:
             quantise(codes1[:, piece], scales1[:, piece], in1[:, piece, :])
-        firsts = [tile([P, P], F32, f"first{t}") for t in range(2)]
-        for t in range(2):
-            nc.vector.tensor_tensor(firsts[t][:], first_bank[:, t, :], gates[:, :P], MULT)
-        for t in range(2):
-            nc.vector.tensor_tensor(windows[t][:].indirect(listed(0, P)), firsts[t][:], windows[3][:, :P], ADD)
+        first_result = tile([P, P], F32, "first_result")
+        nc.vector.tensor_tensor(first_result[:], first_bank[:], gates[:, :P], MULT)
+        nc.vector.tensor_tensor(windows[0][:].indirect(listed(0, P)), first_result[:], windows[3][:, :P], ADD)
 
-        early_banks = [psum.tile([P, GROUP], F32, name="bank") for t in range(NT)]
-        product(early_banks[2][:, :C], 0, 2, codes0[:], scales0[:])
-        product(early_banks[2][:, C:], 1, 2, codes1[:], scales1[:])
-        for t in (0, 1, 3):
-            first = 0 if t == 3 else P
+        second_banks = [psum.tile([P, P], F32, name="bank") for piece in range(4)]
+        for i, piece in enumerate(pieces):
+            product(second_banks[i][:], 0, 1, codes0[:, piece], scales0[:, piece])
+        product(second_banks[2][:], 1, 1, codes1[:, :P], scales1[:, :P])
+        early1 = tile([P, C + P], F32, "early1")
+        for i in range(3):
+            nc.scalar.copy(early1[:, P * i : P * (i + 1)], second_banks[i][:])
+        scatter(1, 0, C + P, early1[:])
+
+        early_banks = {t: psum.tile([P, GROUP], F32, name="bank") for t in (0, 2, 3)}
+        for t in (0, 2, 3):
+            first = P if t == 0 else 0
             product(early_banks[t][:, C:], 1, t, codes1[:], scales1[:])
             product(early_banks[t][:, first:C], 0, t, codes0[:, first:], scales0[:, first:])
-
-        for t in (2, 0, 1):
-            first = 0 if t == 2 else P
+        product(second_banks[3][:], 1, 1, codes1[:, P:], scales1[:, P:])
+        for t in (0, 2):
+            first = P if t == 0 else 0
             result = tile([P, GROUP - first], F32, f"early{t}")
             nc.scalar.copy(result[:], early_banks[t][:, first:])
             scatter(t, first, GROUP, result[:])
@@ -196,9 +200,12 @@ def tile_moe_pln_lin_none_kernel(tc, xT, w_words, w_scales, gate, offs, out):
 
         middle_banks = [group_bank(2, t, codes2, scales2) for t in range(NT)]
         for t in range(2):
-            result = tile([P, GROUP], F32, f"middle{t}")
-            nc.scalar.copy(result[:], middle_banks[t][:])
-            scatter(t, GROUP, 2 * GROUP, result[:])
+            first = GROUP - P * t
+            result = tile([P, 2 * GROUP - first], F32, f"middle{t}")
+            if t == 1:
+                nc.scalar.copy(result[:, :P], second_banks[3][:])
+            nc.scalar.copy(result[:, GROUP - first :], middle_banks[t][:])
+            scatter(t, first, 2 * GROUP, result[:])
         both = tile([P, 2 * GROUP], F32, "both")
         nc.scalar.copy(both[:, :GROUP], middle_banks[3][:])
 

@@ -14,13 +14,14 @@ U8 = mybir.dt.uint8
 FP8X4 = mybir.dt.float8_e4m3fn_x4
 FP4X4 = mybir.dt.float4_e2m1fn_x4
 MULT = mybir.AluOpType.mult
-ADD = mybir.AluOpType.add
 COPY = mybir.ActivationFunctionType.Copy
 
 NT = N // P
 GROUP = 2 * C
 HALF = T // 2
 BLOCK = 2 * P
+LOW_END = GROUP + 6 * P
+HIGH_END = GROUP + 5 * P
 
 
 def tile_moe_pln_lin_none_kernel(tc, xT, w_words, w_scales, gate, offs, out):
@@ -52,6 +53,8 @@ def tile_moe_pln_lin_none_kernel(tc, xT, w_words, w_scales, gate, offs, out):
         nc.vector.tensor_copy(windows[2][:, HALF:], zeros)
         nc.vector.tensor_copy(windows[3][:, :HALF], zeros)
         nc.scalar.activation(windows[3][:, HALF:], zeros, COPY)
+        one = tile([P, 1], F32, "one")
+        nc.vector.memset(one[:], 1.0)
 
         scale_rows = w_scales.bitcast(I32).rearrange("e a q n -> q (e a) n")
         x_rows = xT.rearrange("(p j) w -> p j w", j=4)
@@ -67,167 +70,100 @@ def tile_moe_pln_lin_none_kernel(tc, xT, w_words, w_scales, gate, offs, out):
                         first_plane[32 * quad : 32 * quad + 4].bitcast(I32), scale_rows[4 * quad : 4 * quad + 4, :2]
                     )
 
-        gates = tile([P, SLOTS], F32, "gates")
         word_rows = w_words.bitcast(I32).rearrange("e a p b -> p (e a) b")
-        first_words = tile([P, 2 * BLOCK], U8, "first_words")
-        nc.sync.dma_start(first_words[:].bitcast(I32), word_rows[:, 0, : BLOCK // 2])
-        nc.sync.dma_start(gates[:, :C], gate[:P, :C])
-        words0 = tile([P, 2 * BLOCK], U8, "words0")
-        nc.sync.dma_start(words0[:].bitcast(I32), word_rows[:, 0, BLOCK // 2 :])
-        words1 = tile([P, 2 * N], U8, "words1")
-        nc.sync.dma_start(words1[:].bitcast(I32), word_rows[:, 1, :])
-        nc.sync.dma_start(gates[:, C:GROUP], gate[:P, C:GROUP])
+        first_words = tile([P, 2, 2 * N], U8, "first_words")
+        nc.sync.dma_start(
+            first_words[:].rearrange("p e b -> p (e b)").bitcast(I32).rearrange("p (e b) -> p e b", e=2),
+            word_rows[:, :2, :],
+        )
+        gates = tile([P, SLOTS], F32, "gates")
+        nc.sync.dma_start(gates[:, :GROUP], gate[:P, :GROUP])
         late_words = tile([P, E - 2, 2 * N], U8, "late_words")
         nc.sync.dma_start(
             late_words[:].rearrange("p e b -> p (e b)").bitcast(I32).rearrange("p (e b) -> p e b", e=E - 2),
             word_rows[:, 2:, :],
         )
-        nc.sync.dma_start(gates[:, GROUP:], gate[:P, GROUP:])
         plane_words = wplane[:].rearrange("p e n -> p (e n)").bitcast(I32).rearrange("p (e n) -> p e n", e=E - 2)
         for quad in range(4):
             nc.sync.dma_start(plane_words[32 * quad : 32 * quad + 4], scale_rows[4 * quad : 4 * quad + 4, 2:])
+        nc.sync.dma_start(gates[:, GROUP:], gate[:P, GROUP:])
 
-        def weights(e, t):
-            if e == 0:
-                return (first_words, words0)[t // 2][:, BLOCK * (t % 2) : BLOCK * (t % 2 + 1)]
-            return (words1[:] if e == 1 else late_words[:, e - 2, :])[:, BLOCK * t : BLOCK * (t + 1)]
+        picked = tile([P, SLOTS, 4], BF16, "picked")
+        for j in range(4):
+            end = LOW_END if j < 2 else HIGH_END
+            nc.scalar.activation(picked[:, :GROUP, j], raws[j][:].indirect(listed(0, GROUP)), COPY)
+            nc.vector.tensor_copy(picked[:, GROUP:end, j], raws[j][:].indirect(listed(GROUP, end)))
+            nc.scalar.activation(picked[:, end:, j], raws[j][:].indirect(listed(end, SLOTS)), COPY)
 
-        def quantise(codes, scales, values):
-            nc.vector.quantize_mx(out=codes.bitcast(FP8X4), scales=scales, in_=values.rearrange("p w j -> p (w j)"))
+        codes = tile([P, SLOTS], U32, "codes")
+        scales = tile([P, SLOTS], U8, "scales")
 
-        def product(target, e, t, codes, scales):
-            nc.tensor.matmul_mx(
-                out=target,
-                lhsT=weights(e, t).bitcast(FP4X4),
-                lhsT_scale=(wplane[:, e - 2, :] if e > 1 else first_plane[:, e, :])[:, P * t : P * (t + 1)],
-                rhs=codes.bitcast(FP8X4),
-                rhs_scale=scales,
-                start=True,
-                stop=True,
+        def quantise(first, last):
+            nc.vector.quantize_mx(
+                out=codes[:, first:last].bitcast(FP8X4),
+                scales=scales[:, first:last],
+                in_=picked[:, first:last, :].rearrange("p s j -> p (s j)"),
             )
 
-        def pick(target, j, first, last):
-            nc.scalar.activation(target, raws[j][:].indirect(listed(first, last)), COPY)
-
-        def scatter(t, first, last, values):
-            nc.vector.tensor_tensor(windows[t][:].indirect(listed(first, last)), values, gates[:, first:last], MULT)
-
-        def weave(values, planes):
-            nc.scalar.copy(values, planes.rearrange("p j s -> p s j"))
-
-        in0 = tile([P, C, 4], BF16, "in0")
-        in1 = tile([P, C, 4], BF16, "in1")
-        in2 = tile([P, GROUP, 4], BF16, "in2")
-        low = tile([P, 2, C + GROUP], BF16, "low")
-        planes1 = tile([P, 2, C], BF16, "planes1")
-        for j in range(3):
-            picked = tile([P, C], BF16, f"picked{j}")
-            nc.vector.tensor_copy(picked[:], raws[j][:].indirect(listed(0, C)))
-            nc.vector.tensor_copy(in0[:, :, j], picked[:])
-            if j < 2:
-                pick(low[:, j, :], j, C, 2 * GROUP)
-                nc.vector.tensor_copy(in1[:, :, j], low[:, j, :C])
-                nc.vector.tensor_copy(in2[:, :, j], low[:, j, C:])
-            else:
-                pick(planes1[:, 0, :], j, C, GROUP)
-
-        pieces = [slice(0, P), slice(P, 2 * P)]
-        dense = [tile([P, P], BF16, f"dense{i}") for i in range(2)]
-        for piece, picked in zip(pieces, dense):
-            nc.vector.tensor_copy(picked[:], raws[3][:].indirect(listed(piece.start, piece.stop)))
-        for piece, picked in zip(pieces, dense):
-            nc.vector.tensor_copy(in0[:, piece, 3], picked[:])
-        for piece in pieces:
-            pick(planes1[:, 1, piece], 3, C + piece.start, C + piece.stop)
-        for piece in pieces:
-            weave(in1[:, piece, 2:], planes1[:, :, piece])
-        codes0 = tile([P, C], U32, "codes0")
-        scales0 = tile([P, C], U8, "scales0")
-        quantise(codes0[:, :P], scales0[:, :P], in0[:, :P, :])
-        first_bank = psum.tile([P, P], F32, name="bank")
-        product(first_bank[:], 0, 0, codes0[:, :P], scales0[:, :P])
-        quantise(codes0[:, P:], scales0[:, P:], in0[:, P:, :])
-        codes1 = tile([P, C], U32, "codes1", "chain")
-        scales1 = tile([P, C], U8, "scales1")
-        for piece in pieces:
-            quantise(codes1[:, piece], scales1[:, piece], in1[:, piece, :])
-        first_result = tile([P, P], F32, "first_result")
-        nc.vector.tensor_tensor(first_result[:], first_bank[:], gates[:, :P], MULT)
-        nc.vector.tensor_tensor(windows[0][:].indirect(listed(0, P)), first_result[:], windows[3][:, :P], ADD)
-
-        second_banks = [psum.tile([P, P], F32, name="bank") for piece in range(4)]
-        for i, piece in enumerate(pieces):
-            product(second_banks[i][:], 0, 1, codes0[:, piece], scales0[:, piece])
-        product(second_banks[2][:], 1, 1, codes1[:, :P], scales1[:, :P])
-        early1 = tile([P, C + P], F32, "early1")
-        for i in range(3):
-            nc.scalar.copy(early1[:, P * i : P * (i + 1)], second_banks[i][:])
-        scatter(1, 0, C + P, early1[:])
-
-        early_banks = {t: psum.tile([P, GROUP], F32, name="bank") for t in (0, 2, 3)}
-        for t in (0, 2, 3):
-            first = P if t == 0 else 0
-            product(early_banks[t][:, C:], 1, t, codes1[:], scales1[:])
-            product(early_banks[t][:, first:C], 0, t, codes0[:, first:], scales0[:, first:])
-        product(second_banks[3][:], 1, 1, codes1[:, P:], scales1[:, P:])
-        for t in (0, 2):
-            first = P if t == 0 else 0
-            result = tile([P, GROUP - first], F32, f"early{t}")
-            nc.scalar.copy(result[:], early_banks[t][:, first:])
-            scatter(t, first, GROUP, result[:])
-        planes2 = tile([P, 2, GROUP], BF16, "planes2", "chain")
-        for j in (2, 3):
-            pick(planes2[:, j - 2, :], j, GROUP, 2 * GROUP)
-
-        def group_bank(e, t, codes, scales):
+        def products(t, g):
             bank = psum.tile([P, GROUP], F32, name="bank")
             for half in range(2):
-                cols = slice(C * half, C * (half + 1))
-                product(bank[:, cols], e + half, t, codes[:, cols], scales[:, cols])
+                e = 2 * g + half
+                words = first_words[:, e, :] if e < 2 else late_words[:, e - 2, :]
+                plane = first_plane[:, e, :] if e < 2 else wplane[:, e - 2, :]
+                nc.tensor.matmul_mx(
+                    out=bank[:, C * half : C * (half + 1)],
+                    lhsT=words[:, BLOCK * t : BLOCK * (t + 1)].bitcast(FP4X4),
+                    lhsT_scale=plane[:, P * t : P * (t + 1)],
+                    rhs=codes[:, C * e : C * (e + 1)].bitcast(FP8X4),
+                    rhs_scale=scales[:, C * e : C * (e + 1)],
+                    start=True,
+                    stop=True,
+                )
             return bank
 
-        weave(in2[:, :, 2:], planes2[:])
-        codes2 = tile([P, GROUP], U32, "codes2")
-        scales2 = tile([P, GROUP], U8, "scales2")
-        quantise(codes2[:], scales2[:], in2[:])
-        early3 = tile([P, GROUP], F32, "early3", "chain")
-        nc.scalar.copy(early3[:], early_banks[3][:])
-        scatter(3, 0, GROUP, early3[:])
+        values = [tile([P, SLOTS], F32, f"values{t}") for t in range(NT)]
 
-        planes3 = tile([P, 2, GROUP], BF16, "planes3", "codes0")
-        for j in range(2):
-            pick(planes3[:, j, :], j, 2 * GROUP, SLOTS)
+        def gated(t, g):
+            cols = slice(GROUP * g, GROUP * (g + 1))
+            nc.vector.tensor_tensor(values[t][:, cols], products(t, g)[:], gates[:, cols], MULT)
 
-        middle_banks = [group_bank(2, t, codes2, scales2) for t in range(NT)]
-        for t in range(2):
-            first = GROUP - P * t
-            result = tile([P, 2 * GROUP - first], F32, f"middle{t}")
-            if t == 1:
-                nc.scalar.copy(result[:, :P], second_banks[3][:])
-            nc.scalar.copy(result[:, GROUP - first :], middle_banks[t][:])
-            scatter(t, first, 2 * GROUP, result[:])
-        both = tile([P, 2 * GROUP], F32, "both")
-        nc.scalar.copy(both[:, :GROUP], middle_banks[3][:])
+        def plain(engine_copy, t, g):
+            engine_copy(values[t][:, GROUP * g : GROUP * (g + 1)], products(t, g)[:])
 
-        high3 = tile([P, 2, GROUP], BF16, "high3", "scales2")
-        for j in (2, 3):
-            pick(high3[:, j - 2, :], j, 2 * GROUP, SLOTS)
-        in3 = tile([P, GROUP, 4], BF16, "in3")
-        weave(in3[:, :, :2], planes3[:])
-        weave(in3[:, :, 2:], high3[:])
-        codes3 = tile([P, GROUP], U32, "codes3")
-        scales3 = tile([P, GROUP], U8, "scales3")
-        quantise(codes3[:], scales3[:], in3[:])
-        middle2 = tile([P, GROUP], F32, "middle2", "scales2")
-        nc.scalar.copy(middle2[:], middle_banks[2][:])
-        scatter(2, GROUP, 2 * GROUP, middle2[:])
+        def scalar_scatter(t, first, last):
+            nc.scalar.activation(
+                windows[t][:].indirect(listed(first, last)), values[t][:, first:last], COPY, scale=one[:]
+            )
 
-        for t in range(NT - 1):
-            result = tile([P, GROUP], F32, f"last{t}")
-            nc.scalar.copy(result[:], group_bank(4, t, codes3, scales3)[:])
-            scatter(t, 2 * GROUP, SLOTS, result[:])
-            nc.sync.dma_start(out[P * t : P * (t + 1), :], windows[t][:])
-        nc.scalar.copy(both[:, GROUP:], group_bank(4, 3, codes3, scales3)[:])
-        scatter(3, GROUP, SLOTS, both[:])
+        def vector_scatter(t, first, last):
+            nc.vector.tensor_tensor(
+                windows[t][:].indirect(listed(first, last)), values[t][:, first:last], gates[:, first:last], MULT
+            )
+
+        quantise(0, GROUP)
+        quantise(GROUP, 2 * GROUP)
+        plain(nc.scalar.copy, 2, 0)
+        gated(0, 0)
+        quantise(2 * GROUP, SLOTS)
+        scalar_scatter(0, 0, GROUP)
+        vector_scatter(2, 0, GROUP)
+        for g in (1, 2):
+            plain(nc.scalar.copy, 2, g)
+            gated(0, g)
+        scalar_scatter(0, GROUP, SLOTS)
+        nc.sync.dma_start(out[:P, :], windows[0][:])
+        for g in range(3):
+            gated(1, g)
+        vector_scatter(2, GROUP, SLOTS)
+        nc.sync.dma_start(out[2 * P : 3 * P, :], windows[2][:])
+        plain(nc.scalar.copy, 3, 0)
+        scalar_scatter(1, 0, GROUP)
+        scalar_scatter(1, GROUP, SLOTS)
+        nc.sync.dma_start(out[P : 2 * P, :], windows[1][:])
+        for g in (1, 2):
+            plain(nc.vector.tensor_copy, 3, g)
+        vector_scatter(3, 0, GROUP)
+        vector_scatter(3, GROUP, SLOTS)
         nc.sync.dma_start(out[3 * P :, :HALF], windows[3][:, :HALF])
         nc.scalar.dma_start(out[3 * P :, HALF:], windows[3][:, HALF:])

@@ -20,8 +20,7 @@ NT = N // P
 GROUP = 2 * C
 HALF = T // 2
 BLOCK = 2 * P
-LOW_END = GROUP + 6 * P
-HIGH_END = GROUP + 5 * P
+SPLIT = GROUP + 3 * P
 
 
 def tile_moe_pln_lin_none_kernel(tc, xT, w_words, w_scales, gate, offs, out):
@@ -58,12 +57,10 @@ def tile_moe_pln_lin_none_kernel(tc, xT, w_words, w_scales, gate, offs, out):
 
         scale_rows = w_scales.bitcast(I32).rearrange("e a q n -> q (e a) n")
         x_rows = xT.rearrange("(p j) w -> p j w", j=4)
-        raws = []
-        for j in range(4):
-            raw = tile([P, T], F32, f"raw{j}")
-            nc.sync.dma_start(raw[:], x_rows[:, j, :])
-            raws.append(raw)
-            if j == 0:
+        raws = [tile([P, T], F32, f"raw{j}") for j in range(4)]
+        for j in (2, 0, 1, 3):
+            nc.sync.dma_start(raws[j][:], x_rows[:, j, :])
+            if j == 2:
                 nc.sync.dma_start(offsets[:], offs)
                 for quad in range(4):
                     nc.sync.dma_start(
@@ -71,13 +68,18 @@ def tile_moe_pln_lin_none_kernel(tc, xT, w_words, w_scales, gate, offs, out):
                     )
 
         word_rows = w_words.bitcast(I32).rearrange("e a p b -> p (e a) b")
-        first_words = tile([P, 2, 2 * N], U8, "first_words")
+        first_words = tile([P, 2, BLOCK], U8, "first_words", "reused")
         nc.sync.dma_start(
             first_words[:].rearrange("p e b -> p (e b)").bitcast(I32).rearrange("p (e b) -> p e b", e=2),
-            word_rows[:, :2, :],
+            word_rows[:, :2, : BLOCK // 4],
         )
         gates = tile([P, SLOTS], F32, "gates")
         nc.sync.dma_start(gates[:, :GROUP], gate[:P, :GROUP])
+        early_words = tile([P, 2, 3 * BLOCK], U8, "early_words")
+        nc.sync.dma_start(
+            early_words[:].rearrange("p e b -> p (e b)").bitcast(I32).rearrange("p (e b) -> p e b", e=2),
+            word_rows[:, :2, BLOCK // 4 :],
+        )
         late_words = tile([P, E - 2, 2 * N], U8, "late_words")
         nc.sync.dma_start(
             late_words[:].rearrange("p e b -> p (e b)").bitcast(I32).rearrange("p (e b) -> p e b", e=E - 2),
@@ -88,35 +90,49 @@ def tile_moe_pln_lin_none_kernel(tc, xT, w_words, w_scales, gate, offs, out):
             nc.sync.dma_start(plane_words[32 * quad : 32 * quad + 4], scale_rows[4 * quad : 4 * quad + 4, 2:])
         nc.sync.dma_start(gates[:, GROUP:], gate[:P, GROUP:])
 
-        picked = tile([P, SLOTS, 4], BF16, "picked")
-        for j in range(4):
-            end = LOW_END if j < 2 else HIGH_END
-            nc.scalar.activation(picked[:, :GROUP, j], raws[j][:].indirect(listed(0, GROUP)), COPY)
-            nc.vector.tensor_copy(picked[:, GROUP:end, j], raws[j][:].indirect(listed(GROUP, end)))
-            nc.scalar.activation(picked[:, end:, j], raws[j][:].indirect(listed(end, SLOTS)), COPY)
+        early = tile([P, GROUP, 4], BF16, "early")
+        rest = tile([P, 2 * GROUP, 4], BF16, "rest")
+
+        def scalar_gather(j, first, last):
+            nc.scalar.activation(rest[:, first - GROUP : last - GROUP, j], raws[j][:].indirect(listed(first, last)), COPY)
+
+        for j in (2, 0, 1, 3):
+            nc.vector.tensor_copy(early[:, :, j], raws[j][:].indirect(listed(0, GROUP)))
+            if j < 2:
+                nc.vector.tensor_copy(rest[:, : SPLIT - GROUP, j], raws[j][:].indirect(listed(GROUP, SPLIT)))
+                scalar_gather(j, SPLIT, SLOTS)
+            elif j == 2:
+                scalar_gather(j, GROUP, SLOTS)
+            else:
+                scalar_gather(j, GROUP, 2 * GROUP)
+                scalar_gather(j, 2 * GROUP, SLOTS)
 
         codes = tile([P, SLOTS], U32, "codes")
-        scales = tile([P, SLOTS], U8, "scales")
+        scales = [tile([P, GROUP], U8, f"scales{g}", "reused" if g == 2 else None) for g in range(3)]
 
-        def quantise(first, last):
+        def quantise(first, last, source):
             nc.vector.quantize_mx(
                 out=codes[:, first:last].bitcast(FP8X4),
-                scales=scales[:, first:last],
-                in_=picked[:, first:last, :].rearrange("p s j -> p (s j)"),
+                scales=scales[first // GROUP][:, first % GROUP : (last - 1) % GROUP + 1],
+                in_=source.rearrange("p s j -> p (s j)"),
             )
+
+        def weights(e, t):
+            if e > 1:
+                return late_words[:, e - 2, BLOCK * t : BLOCK * (t + 1)]
+            return first_words[:, e, :] if t == 0 else early_words[:, e, BLOCK * (t - 1) : BLOCK * t]
 
         def products(t, g):
             bank = psum.tile([P, GROUP], F32, name="bank")
             for half in range(2):
                 e = 2 * g + half
-                words = first_words[:, e, :] if e < 2 else late_words[:, e - 2, :]
                 plane = first_plane[:, e, :] if e < 2 else wplane[:, e - 2, :]
                 nc.tensor.matmul_mx(
                     out=bank[:, C * half : C * (half + 1)],
-                    lhsT=words[:, BLOCK * t : BLOCK * (t + 1)].bitcast(FP4X4),
+                    lhsT=weights(e, t).bitcast(FP4X4),
                     lhsT_scale=plane[:, P * t : P * (t + 1)],
                     rhs=codes[:, C * e : C * (e + 1)].bitcast(FP8X4),
-                    rhs_scale=scales[:, C * e : C * (e + 1)],
+                    rhs_scale=scales[e // 2][:, C * (e % 2) : C * (e % 2 + 1)],
                     start=True,
                     stop=True,
                 )
@@ -141,29 +157,30 @@ def tile_moe_pln_lin_none_kernel(tc, xT, w_words, w_scales, gate, offs, out):
                 windows[t][:].indirect(listed(first, last)), values[t][:, first:last], gates[:, first:last], MULT
             )
 
-        quantise(0, GROUP)
-        quantise(GROUP, 2 * GROUP)
-        plain(nc.scalar.copy, 2, 0)
+        quantise(0, C, early[:, :C, :])
+        quantise(C, GROUP, early[:, C:, :])
+        quantise(GROUP, 2 * GROUP, rest[:, :GROUP, :])
         gated(0, 0)
-        quantise(2 * GROUP, SLOTS)
+        plain(nc.vector.tensor_copy, 2, 0)
+        quantise(2 * GROUP, SLOTS, rest[:, GROUP:, :])
         scalar_scatter(0, 0, GROUP)
         vector_scatter(2, 0, GROUP)
-        for g in (1, 2):
-            plain(nc.scalar.copy, 2, g)
-            gated(0, g)
+        for t, g in ((3, 0), (2, 1), (3, 1)):
+            plain(nc.scalar.copy, t, g)
+        gated(1, 0)
+        scalar_scatter(1, 0, GROUP)
+        for t in (0, 1):
+            for g in (1, 2):
+                gated(t, g)
+        plain(nc.vector.tensor_copy, 3, 2)
+        plain(nc.vector.tensor_copy, 2, 2)
+        vector_scatter(3, 2 * GROUP, SLOTS)
         scalar_scatter(0, GROUP, SLOTS)
         nc.sync.dma_start(out[:P, :], windows[0][:])
-        for g in range(3):
-            gated(1, g)
         vector_scatter(2, GROUP, SLOTS)
         nc.sync.dma_start(out[2 * P : 3 * P, :], windows[2][:])
-        plain(nc.scalar.copy, 3, 0)
-        scalar_scatter(1, 0, GROUP)
         scalar_scatter(1, GROUP, SLOTS)
-        nc.sync.dma_start(out[P : 2 * P, :], windows[1][:])
-        for g in (1, 2):
-            plain(nc.vector.tensor_copy, 3, g)
-        vector_scatter(3, 0, GROUP)
-        vector_scatter(3, GROUP, SLOTS)
+        nc.scalar.dma_start(out[P : 2 * P, :], windows[1][:])
+        vector_scatter(3, 0, 2 * GROUP)
         nc.sync.dma_start(out[3 * P :, :HALF], windows[3][:, :HALF])
         nc.scalar.dma_start(out[3 * P :, HALF:], windows[3][:, HALF:])

@@ -20,7 +20,7 @@ NT = N // P
 GROUP = 2 * C
 HALF = T // 2
 BLOCK = 2 * P
-SPLIT = GROUP + 3 * P
+FIRST = 3 * P
 
 
 def tile_moe_pln_lin_none_kernel(tc, xT, w_words, w_scales, gate, offs, out):
@@ -52,8 +52,6 @@ def tile_moe_pln_lin_none_kernel(tc, xT, w_words, w_scales, gate, offs, out):
         nc.vector.tensor_copy(windows[2][:, HALF:], zeros)
         nc.vector.tensor_copy(windows[3][:, :HALF], zeros)
         nc.scalar.activation(windows[3][:, HALF:], zeros, COPY)
-        one = tile([P, 1], F32, "one")
-        nc.vector.memset(one[:], 1.0)
 
         scale_rows = w_scales.bitcast(I32).rearrange("e a q n -> q (e a) n")
         x_rows = xT.rearrange("(p j) w -> p j w", j=4)
@@ -68,17 +66,17 @@ def tile_moe_pln_lin_none_kernel(tc, xT, w_words, w_scales, gate, offs, out):
                     )
 
         word_rows = w_words.bitcast(I32).rearrange("e a p b -> p (e a) b")
-        first_words = tile([P, 2, BLOCK], U8, "first_words", "reused")
+        first_words = tile([P, 2, 2 * BLOCK], U8, "first_words", "reused")
         nc.sync.dma_start(
             first_words[:].rearrange("p e b -> p (e b)").bitcast(I32).rearrange("p (e b) -> p e b", e=2),
-            word_rows[:, :2, : BLOCK // 4],
+            word_rows[:, :2, : BLOCK // 2],
         )
         gates = tile([P, SLOTS], F32, "gates")
         nc.sync.dma_start(gates[:, :GROUP], gate[:P, :GROUP])
-        early_words = tile([P, 2, 3 * BLOCK], U8, "early_words")
+        early_words = tile([P, 2, 2 * BLOCK], U8, "early_words")
         nc.sync.dma_start(
             early_words[:].rearrange("p e b -> p (e b)").bitcast(I32).rearrange("p (e b) -> p e b", e=2),
-            word_rows[:, :2, BLOCK // 4 :],
+            word_rows[:, :2, BLOCK // 2 :],
         )
         late_words = tile([P, E - 2, 2 * N], U8, "late_words")
         nc.sync.dma_start(
@@ -90,37 +88,34 @@ def tile_moe_pln_lin_none_kernel(tc, xT, w_words, w_scales, gate, offs, out):
             nc.sync.dma_start(plane_words[32 * quad : 32 * quad + 4], scale_rows[4 * quad : 4 * quad + 4, 2:])
         nc.sync.dma_start(gates[:, GROUP:], gate[:P, GROUP:])
 
-        early = tile([P, GROUP, 4], BF16, "early")
-        rest = tile([P, 2 * GROUP, 4], BF16, "rest")
+        picked = tile([P, SLOTS, 4], BF16, "picked")
 
-        def scalar_gather(j, first, last):
-            nc.scalar.activation(rest[:, first - GROUP : last - GROUP, j], raws[j][:].indirect(listed(first, last)), COPY)
+        def vector_gather(j, last):
+            nc.vector.tensor_copy(picked[:, :last, j], raws[j][:].indirect(listed(0, last)))
 
-        for j in (2, 0, 1, 3):
-            nc.vector.tensor_copy(early[:, :, j], raws[j][:].indirect(listed(0, GROUP)))
-            if j < 2:
-                nc.vector.tensor_copy(rest[:, : SPLIT - GROUP, j], raws[j][:].indirect(listed(GROUP, SPLIT)))
-                scalar_gather(j, SPLIT, SLOTS)
-            elif j == 2:
-                scalar_gather(j, GROUP, SLOTS)
-            else:
-                scalar_gather(j, GROUP, 2 * GROUP)
-                scalar_gather(j, 2 * GROUP, SLOTS)
+        for j in (2, 0, 1):
+            vector_gather(j, SLOTS // 2)
+            nc.scalar.activation(picked[:, SLOTS // 2 :, j], raws[j][:].indirect(listed(SLOTS // 2, SLOTS)), COPY)
+        one = tile([P, 1], F32, "one", "raw2")
+        nc.vector.memset(one[:], 1.0)
+        vector_gather(3, FIRST)
+        for first, last in ((FIRST, GROUP), (GROUP, 2 * GROUP), (2 * GROUP, SLOTS)):
+            nc.scalar.activation(picked[:, first:last, 3], raws[3][:].indirect(listed(first, last)), COPY, scale=one[:])
 
         codes = tile([P, SLOTS], U32, "codes")
         scales = [tile([P, GROUP], U8, f"scales{g}", "reused" if g == 2 else None) for g in range(3)]
 
-        def quantise(first, last, source):
+        def quantise(first, last):
             nc.vector.quantize_mx(
                 out=codes[:, first:last].bitcast(FP8X4),
                 scales=scales[first // GROUP][:, first % GROUP : (last - 1) % GROUP + 1],
-                in_=source.rearrange("p s j -> p (s j)"),
+                in_=picked[:, first:last, :].rearrange("p s j -> p (s j)"),
             )
 
         def weights(e, t):
             if e > 1:
                 return late_words[:, e - 2, BLOCK * t : BLOCK * (t + 1)]
-            return first_words[:, e, :] if t == 0 else early_words[:, e, BLOCK * (t - 1) : BLOCK * t]
+            return (first_words, early_words)[t // 2][:, e, BLOCK * (t % 2) : BLOCK * (t % 2 + 1)]
 
         def products(t, g):
             bank = psum.tile([P, GROUP], F32, name="bank")
@@ -157,30 +152,30 @@ def tile_moe_pln_lin_none_kernel(tc, xT, w_words, w_scales, gate, offs, out):
                 windows[t][:].indirect(listed(first, last)), values[t][:, first:last], gates[:, first:last], MULT
             )
 
-        quantise(0, C, early[:, :C, :])
-        quantise(C, GROUP, early[:, C:, :])
-        quantise(GROUP, 2 * GROUP, rest[:, :GROUP, :])
+        quantise(0, C)
+        quantise(C, GROUP)
+        quantise(GROUP, 2 * GROUP)
         gated(0, 0)
-        plain(nc.vector.tensor_copy, 2, 0)
-        quantise(2 * GROUP, SLOTS, rest[:, GROUP:, :])
+        plain(nc.vector.tensor_copy, 1, 0)
+        quantise(2 * GROUP, SLOTS)
         scalar_scatter(0, 0, GROUP)
-        vector_scatter(2, 0, GROUP)
-        for t, g in ((3, 0), (2, 1), (3, 1)):
+        vector_scatter(1, 0, GROUP)
+        for t, g in ((3, 0), (1, 1), (3, 1)):
             plain(nc.scalar.copy, t, g)
-        gated(1, 0)
-        scalar_scatter(1, 0, GROUP)
-        for t in (0, 1):
+        gated(2, 0)
+        scalar_scatter(2, 0, GROUP)
+        for t in (0, 2):
             for g in (1, 2):
                 gated(t, g)
         plain(nc.vector.tensor_copy, 3, 2)
-        plain(nc.vector.tensor_copy, 2, 2)
+        plain(nc.vector.tensor_copy, 1, 2)
         vector_scatter(3, 2 * GROUP, SLOTS)
         scalar_scatter(0, GROUP, SLOTS)
         nc.sync.dma_start(out[:P, :], windows[0][:])
-        vector_scatter(2, GROUP, SLOTS)
-        nc.sync.dma_start(out[2 * P : 3 * P, :], windows[2][:])
-        scalar_scatter(1, GROUP, SLOTS)
-        nc.scalar.dma_start(out[P : 2 * P, :], windows[1][:])
+        vector_scatter(1, GROUP, SLOTS)
+        nc.sync.dma_start(out[P : 2 * P, :], windows[1][:])
+        scalar_scatter(2, GROUP, SLOTS)
+        nc.scalar.dma_start(out[2 * P : 3 * P, :], windows[2][:])
         vector_scatter(3, 0, 2 * GROUP)
         nc.sync.dma_start(out[3 * P :, :HALF], windows[3][:, :HALF])
         nc.scalar.dma_start(out[3 * P :, HALF:], windows[3][:, HALF:])

@@ -20,7 +20,8 @@ NT = N // P
 GROUP = 2 * C
 HALF = T // 2
 BLOCK = 2 * P
-FIRST = 3 * P
+HEAD_SPLIT = 736
+LAST_SPLIT = C + 3 * P
 
 
 def tile_moe_pln_lin_none_kernel(tc, xT, w_words, w_scales, gate, offs, out):
@@ -90,16 +91,16 @@ def tile_moe_pln_lin_none_kernel(tc, xT, w_words, w_scales, gate, offs, out):
 
         picked = tile([P, SLOTS, 4], BF16, "picked")
 
-        def vector_gather(j, last):
-            nc.vector.tensor_copy(picked[:, :last, j], raws[j][:].indirect(listed(0, last)))
+        def vector_gather(j, first, last):
+            nc.vector.tensor_copy(picked[:, first:last, j], raws[j][:].indirect(listed(first, last)))
 
         for j in (2, 0, 1):
-            vector_gather(j, SLOTS // 2)
-            nc.scalar.activation(picked[:, SLOTS // 2 :, j], raws[j][:].indirect(listed(SLOTS // 2, SLOTS)), COPY)
+            vector_gather(j, 0, HEAD_SPLIT)
+            nc.scalar.activation(picked[:, HEAD_SPLIT:, j], raws[j][:].indirect(listed(HEAD_SPLIT, SLOTS)), COPY)
         one = tile([P, 1], F32, "one", "raw2")
         nc.vector.memset(one[:], 1.0)
-        vector_gather(3, FIRST)
-        for first, last in ((FIRST, GROUP), (GROUP, 2 * GROUP), (2 * GROUP, SLOTS)):
+        vector_gather(3, C, LAST_SPLIT)
+        for first, last in ((0, C), (LAST_SPLIT, 2 * GROUP), (2 * GROUP, SLOTS)):
             nc.scalar.activation(picked[:, first:last, 3], raws[3][:].indirect(listed(first, last)), COPY, scale=one[:])
 
         codes = tile([P, SLOTS], U32, "codes")
@@ -119,7 +120,7 @@ def tile_moe_pln_lin_none_kernel(tc, xT, w_words, w_scales, gate, offs, out):
 
         def products(t, g):
             bank = psum.tile([P, GROUP], F32, name="bank")
-            for half in range(2):
+            for half in (1, 0) if (t, g) == (0, 0) else (0, 1):
                 e = 2 * g + half
                 plane = first_plane[:, e, :] if e < 2 else wplane[:, e - 2, :]
                 nc.tensor.matmul_mx(
@@ -152,8 +153,8 @@ def tile_moe_pln_lin_none_kernel(tc, xT, w_words, w_scales, gate, offs, out):
                 windows[t][:].indirect(listed(first, last)), values[t][:, first:last], gates[:, first:last], MULT
             )
 
-        quantise(0, C)
         quantise(C, GROUP)
+        quantise(0, C)
         quantise(GROUP, 2 * GROUP)
         gated(0, 0)
         plain(nc.vector.tensor_copy, 1, 0)

@@ -61,10 +61,10 @@ def tile_moe_pln_lin_none_kernel(tc, xT, w_words, w_scales, gate, offs, out):
             nc.sync.dma_start(raws[j][:], x_rows[:, j, :])
             if j == 2:
                 nc.sync.dma_start(offsets[:], offs)
-                for quad in range(4):
-                    nc.sync.dma_start(
-                        first_plane[32 * quad : 32 * quad + 4].bitcast(I32), scale_rows[4 * quad : 4 * quad + 4, :2]
-                    )
+        for quad in range(4):
+            nc.sync.dma_start(
+                first_plane[32 * quad : 32 * quad + 4].bitcast(I32), scale_rows[4 * quad : 4 * quad + 4, :2]
+            )
 
         word_rows = w_words.bitcast(I32).rearrange("e a p b -> p (e a) b")
         first_words = tile([P, 2, 2 * BLOCK], U8, "first_words", "reused")

@@ -28,7 +28,7 @@ def tile_moe_pln_lin_none_kernel(tc, xT, w_words, w_scales, gate, offs, out):
     nc = tc.nc
     with (
         tc.tile_pool(name="held", bufs=1) as held,
-        tc.psum_pool(name="psum", bufs=8) as psum,
+        tc.psum_pool(name="psum", bufs=4) as psum,
     ):
         def tile(shape, dtype, name, tag=None):
             return held.tile(shape, dtype, name=name, tag=tag or name, align_bytes=64)
@@ -118,10 +118,10 @@ def tile_moe_pln_lin_none_kernel(tc, xT, w_words, w_scales, gate, offs, out):
                 return late_words[:, e - 2, BLOCK * t : BLOCK * (t + 1)]
             return (first_words, early_words)[t // 2][:, e, BLOCK * (t % 2) : BLOCK * (t % 2 + 1)]
 
-        def products(t, g):
-            bank = psum.tile([P, GROUP], F32, name="bank")
-            for half in (1, 0) if (t, g) == (0, 0) else (0, 1):
-                e = 2 * g + half
+        def products(t, experts, reader):
+            bank = psum.tile([P, C * len(experts)], F32, name=reader)
+            for e in experts:
+                half = e - min(experts)
                 plane = first_plane[:, e, :] if e < 2 else wplane[:, e - 2, :]
                 nc.tensor.matmul_mx(
                     out=bank[:, C * half : C * (half + 1)],
@@ -136,12 +136,18 @@ def tile_moe_pln_lin_none_kernel(tc, xT, w_words, w_scales, gate, offs, out):
 
         values = [tile([P, SLOTS], F32, f"values{t}") for t in range(NT)]
 
-        def gated(t, g):
-            cols = slice(GROUP * g, GROUP * (g + 1))
-            nc.vector.tensor_tensor(values[t][:, cols], products(t, g)[:], gates[:, cols], MULT)
+        def columns(experts):
+            return slice(C * min(experts), C * (max(experts) + 1))
 
-        def plain(engine_copy, t, g):
-            engine_copy(values[t][:, GROUP * g : GROUP * (g + 1)], products(t, g)[:])
+        def gated(t, experts):
+            cols = columns(experts)
+            nc.vector.tensor_tensor(values[t][:, cols], products(t, experts, "vector")[:], gates[:, cols], MULT)
+
+        def vector_copy(t, experts):
+            nc.vector.tensor_copy(values[t][:, columns(experts)], products(t, experts, "vector")[:])
+
+        def scalar_copy(t, experts):
+            nc.scalar.copy(values[t][:, columns(experts)], products(t, experts, "scalar")[:])
 
         def scalar_scatter(t, first, last):
             nc.scalar.activation(
@@ -156,20 +162,20 @@ def tile_moe_pln_lin_none_kernel(tc, xT, w_words, w_scales, gate, offs, out):
         quantise(C, GROUP)
         quantise(0, C)
         quantise(GROUP, 2 * GROUP)
-        gated(0, 0)
-        plain(nc.vector.tensor_copy, 1, 0)
+        gated(0, (1, 0))
+        vector_copy(1, (0, 1))
         quantise(2 * GROUP, SLOTS)
+        gated(2, (0, 1))
         scalar_scatter(0, 0, GROUP)
         vector_scatter(1, 0, GROUP)
-        for t, g in ((3, 0), (1, 1), (3, 1)):
-            plain(nc.scalar.copy, t, g)
-        gated(2, 0)
+        for t, experts in ((3, (0, 1)), (1, (2, 3)), (3, (2, 3)), (1, (4,))):
+            scalar_copy(t, experts)
         scalar_scatter(2, 0, GROUP)
         for t in (0, 2):
-            for g in (1, 2):
-                gated(t, g)
-        plain(nc.vector.tensor_copy, 3, 2)
-        plain(nc.vector.tensor_copy, 1, 2)
+            for experts in ((2, 3), (4, 5)):
+                gated(t, experts)
+        vector_copy(3, (4, 5))
+        vector_copy(1, (5,))
         vector_scatter(3, 2 * GROUP, SLOTS)
         scalar_scatter(0, GROUP, SLOTS)
         nc.sync.dma_start(out[:P, :], windows[0][:])

@@ -21,7 +21,8 @@ GROUP = 2 * C
 HALF = T // 2
 BLOCK = 2 * P
 HEAD_SPLIT = 736
-LAST_SPLIT = C + 3 * P
+COPY_SPLIT = 2 * GROUP + P
+LAST_FIRST = HEAD_SPLIT - 3 * P
 
 
 def tile_moe_pln_lin_none_kernel(tc, xT, w_words, w_scales, gate, offs, out):
@@ -99,8 +100,8 @@ def tile_moe_pln_lin_none_kernel(tc, xT, w_words, w_scales, gate, offs, out):
             nc.scalar.activation(picked[:, HEAD_SPLIT:, j], raws[j][:].indirect(listed(HEAD_SPLIT, SLOTS)), COPY)
         one = tile([P, 1], F32, "one", "raw2")
         nc.vector.memset(one[:], 1.0)
-        vector_gather(3, C, LAST_SPLIT)
-        for first, last in ((0, C), (LAST_SPLIT, 2 * GROUP), (2 * GROUP, SLOTS)):
+        vector_gather(3, LAST_FIRST, HEAD_SPLIT)
+        for first, last in ((0, C), (C, LAST_FIRST), (HEAD_SPLIT, 2 * GROUP), (2 * GROUP, SLOTS)):
             nc.scalar.activation(picked[:, first:last, 3], raws[3][:].indirect(listed(first, last)), COPY, scale=one[:])
 
         codes = tile([P, SLOTS], U32, "codes")
@@ -118,17 +119,18 @@ def tile_moe_pln_lin_none_kernel(tc, xT, w_words, w_scales, gate, offs, out):
                 return late_words[:, e - 2, BLOCK * t : BLOCK * (t + 1)]
             return (first_words, early_words)[t // 2][:, e, BLOCK * (t % 2) : BLOCK * (t % 2 + 1)]
 
-        def products(t, experts, reader):
-            bank = psum.tile([P, C * len(experts)], F32, name=reader)
-            for e in experts:
-                half = e - min(experts)
+        def products(t, first, last, reader, backwards=False):
+            bank = psum.tile([P, last - first], F32, name=reader)
+            experts = range(first // C, (last - 1) // C + 1)
+            for e in reversed(experts) if backwards else experts:
+                low, high = max(first, C * e), min(last, C * (e + 1))
                 plane = first_plane[:, e, :] if e < 2 else wplane[:, e - 2, :]
                 nc.tensor.matmul_mx(
-                    out=bank[:, C * half : C * (half + 1)],
+                    out=bank[:, low - first : high - first],
                     lhsT=weights(e, t).bitcast(FP4X4),
                     lhsT_scale=plane[:, P * t : P * (t + 1)],
-                    rhs=codes[:, C * e : C * (e + 1)].bitcast(FP8X4),
-                    rhs_scale=scales[e // 2][:, C * (e % 2) : C * (e % 2 + 1)],
+                    rhs=codes[:, low:high].bitcast(FP8X4),
+                    rhs_scale=scales[low // GROUP][:, low % GROUP : (high - 1) % GROUP + 1],
                     start=True,
                     stop=True,
                 )
@@ -136,18 +138,15 @@ def tile_moe_pln_lin_none_kernel(tc, xT, w_words, w_scales, gate, offs, out):
 
         values = [tile([P, SLOTS], F32, f"values{t}") for t in range(NT)]
 
-        def columns(experts):
-            return slice(C * min(experts), C * (max(experts) + 1))
+        def gated(t, first, last, backwards=False):
+            bank = products(t, first, last, "vector", backwards)
+            nc.vector.tensor_tensor(values[t][:, first:last], bank[:], gates[:, first:last], MULT)
 
-        def gated(t, experts):
-            cols = columns(experts)
-            nc.vector.tensor_tensor(values[t][:, cols], products(t, experts, "vector")[:], gates[:, cols], MULT)
+        def vector_copy(t, first, last, backwards=False):
+            nc.vector.tensor_copy(values[t][:, first:last], products(t, first, last, "vector", backwards)[:])
 
-        def vector_copy(t, experts):
-            nc.vector.tensor_copy(values[t][:, columns(experts)], products(t, experts, "vector")[:])
-
-        def scalar_copy(t, experts):
-            nc.scalar.copy(values[t][:, columns(experts)], products(t, experts, "scalar")[:])
+        def scalar_copy(t, first, last, backwards=False):
+            nc.scalar.copy(values[t][:, first:last], products(t, first, last, "scalar", backwards)[:])
 
         def scalar_scatter(t, first, last):
             nc.scalar.activation(
@@ -159,23 +158,25 @@ def tile_moe_pln_lin_none_kernel(tc, xT, w_words, w_scales, gate, offs, out):
                 windows[t][:].indirect(listed(first, last)), values[t][:, first:last], gates[:, first:last], MULT
             )
 
-        quantise(C, GROUP)
         quantise(0, C)
+        quantise(C, GROUP)
         quantise(GROUP, 2 * GROUP)
-        gated(0, (1, 0))
-        vector_copy(1, (0, 1))
+        gated(0, 0, GROUP)
+        vector_copy(1, 0, GROUP, True)
         quantise(2 * GROUP, SLOTS)
-        gated(2, (0, 1))
+        gated(2, 0, GROUP, True)
         scalar_scatter(0, 0, GROUP)
         vector_scatter(1, 0, GROUP)
-        for t, experts in ((3, (0, 1)), (1, (2, 3)), (3, (2, 3)), (1, (4,))):
-            scalar_copy(t, experts)
+        scalar_copy(3, 0, GROUP, True)
+        scalar_copy(1, GROUP, 2 * GROUP)
+        scalar_copy(3, GROUP, 2 * GROUP)
+        scalar_copy(1, 2 * GROUP, COPY_SPLIT)
         scalar_scatter(2, 0, GROUP)
         for t in (0, 2):
-            for experts in ((2, 3), (4, 5)):
-                gated(t, experts)
-        vector_copy(3, (4, 5))
-        vector_copy(1, (5,))
+            for first in (GROUP, 2 * GROUP):
+                gated(t, first, first + GROUP)
+        vector_copy(3, 2 * GROUP, SLOTS)
+        vector_copy(1, COPY_SPLIT, SLOTS)
         vector_scatter(3, 2 * GROUP, SLOTS)
         scalar_scatter(0, GROUP, SLOTS)
         nc.sync.dma_start(out[:P, :], windows[0][:])

@@ -183,7 +183,8 @@ def tile_moe_pln_lin_none_kernel(tc, xT, w_words, w_scales, gate, offs, out):
         vector_scatter(1, GROUP, SLOTS)
         nc.sync.dma_start(out[P : 2 * P, :], windows[1][:])
         scalar_scatter(2, GROUP, SLOTS)
-        nc.scalar.dma_start(out[2 * P : 3 * P, :], windows[2][:])
+        nc.scalar.dma_start(out[2 * P : 3 * P, :HALF], windows[2][:, :HALF])
+        nc.sync.dma_start(out[2 * P : 3 * P, HALF:], windows[2][:, HALF:])
         vector_scatter(3, 0, 2 * GROUP)
         nc.sync.dma_start(out[3 * P :, :HALF], windows[3][:, :HALF])
         nc.scalar.dma_start(out[3 * P :, HALF:], windows[3][:, HALF:])

@@ -42,7 +42,7 @@ def tile_moe_pln_lin_none_kernel(tc, xT, w_words, w_scales, gate, offs, out):
         first_plane = tile([P, 2, N], U8, "first_plane")
         nc.vector.memset(first_plane[:].bitcast(I32), 0)
         wplane = tile([P, E - 2, N], U8, "wplane")
-        windows = [tile([P, T], F32, f"window{t}") for t in range(NT)]
+        windows = [tile([P, T], F32, f"window{t}") for t in range(NT - 1)]
 
         nc.vector.memset(wplane[:].rearrange("p e n -> p (e n)").bitcast(I32), 0)
         zeros = windows[0][:, :HALF]
@@ -52,8 +52,6 @@ def tile_moe_pln_lin_none_kernel(tc, xT, w_words, w_scales, gate, offs, out):
         nc.vector.tensor_copy(windows[1][:, :HALF], zeros)
         nc.vector.tensor_copy(windows[2][:, :HALF], zeros)
         nc.vector.tensor_copy(windows[2][:, HALF:], zeros)
-        nc.vector.tensor_copy(windows[3][:, :HALF], zeros)
-        nc.scalar.activation(windows[3][:, HALF:], zeros, COPY)
 
         scale_rows = w_scales.bitcast(I32).rearrange("e a q n -> q (e a) n")
         x_rows = xT.rearrange("(p j) w -> p j w", j=4)
@@ -164,6 +162,8 @@ def tile_moe_pln_lin_none_kernel(tc, xT, w_words, w_scales, gate, offs, out):
         gated(0, 0, GROUP)
         vector_copy(1, 0, GROUP, True)
         quantise(2 * GROUP, SLOTS)
+        windows.append(tile([P, T], F32, "window3", "picked"))
+        nc.gpsimd.memset(windows[3][:], 0.0)
         gated(2, 0, GROUP, True)
         scalar_scatter(0, 0, GROUP)
         vector_scatter(1, 0, GROUP)

@@ -22,7 +22,8 @@ HALF = T // 2
 BLOCK = 2 * P
 HEAD_SPLIT = 736
 COPY_SPLIT = 2 * GROUP + P
-LAST_FIRST = HEAD_SPLIT - 3 * P
+LAST_FIRST = 352
+LAST_END = 3 * C
 
 
 def tile_moe_pln_lin_none_kernel(tc, xT, w_words, w_scales, gate, offs, out):
@@ -98,8 +99,8 @@ def tile_moe_pln_lin_none_kernel(tc, xT, w_words, w_scales, gate, offs, out):
             nc.scalar.activation(picked[:, HEAD_SPLIT:, j], raws[j][:].indirect(listed(HEAD_SPLIT, SLOTS)), COPY)
         one = tile([P, 1], F32, "one", "raw2")
         nc.vector.memset(one[:], 1.0)
-        vector_gather(3, LAST_FIRST, HEAD_SPLIT)
-        for first, last in ((0, C), (C, LAST_FIRST), (HEAD_SPLIT, 2 * GROUP), (2 * GROUP, SLOTS)):
+        vector_gather(3, LAST_FIRST, LAST_END)
+        for first, last in ((0, C), (C, LAST_FIRST), (LAST_END, 2 * GROUP), (2 * GROUP, SLOTS)):
             nc.scalar.activation(picked[:, first:last, 3], raws[3][:].indirect(listed(first, last)), COPY, scale=one[:])
 
         codes = tile([P, SLOTS], U32, "codes")

import concourse.mybir as mybir

K, T, E, C, N = 512, 2560, 6, 256, 512
P = 128
SLOTS = E * C
FLOPS = 2 * K * N * SLOTS

F32 = mybir.dt.float32
BF16 = mybir.dt.bfloat16
I32 = mybir.dt.int32
U32 = mybir.dt.uint32
U16 = mybir.dt.uint16
U8 = mybir.dt.uint8
FP8X4 = mybir.dt.float8_e4m3fn_x4
FP4X4 = mybir.dt.float4_e2m1fn_x4
MULT = mybir.AluOpType.mult
COPY = mybir.ActivationFunctionType.Copy

NT = N // P
GROUP = 2 * C
HALF = T // 2
BLOCK = 2 * P
HEAD_SPLIT = 736
COPY_SPLIT = 2 * GROUP + P
LAST_FIRST = 352
LAST_END = 3 * C


def tile_moe_pln_lin_none_kernel(tc, xT, w_words, w_scales, gate, offs, out):
    nc = tc.nc
    with (
        tc.tile_pool(name="held", bufs=1) as held,
        tc.psum_pool(name="psum", bufs=4) as psum,
    ):
        def tile(shape, dtype, name, tag=None):
            return held.tile(shape, dtype, name=name, tag=tag or name, align_bytes=64)

        offsets = held.tile([P, SLOTS // 16], U16, name="offsets")

        def listed(first, last):
            return offsets[:, first // 16 : last // 16]

        first_plane = tile([P, 2, N], U8, "first_plane")
        nc.vector.memset(first_plane[:].bitcast(I32), 0)
        wplane = tile([P, E - 2, N], U8, "wplane")
        windows = [tile([P, T], F32, f"window{t}") for t in range(NT - 1)]

        nc.vector.memset(wplane[:].rearrange("p e n -> p (e n)").bitcast(I32), 0)
        zeros = windows[0][:, :HALF]
        nc.vector.memset(zeros.bitcast(I32), 0)
        nc.scalar.activation(windows[1][:, HALF:], zeros, COPY)
        nc.vector.tensor_copy(windows[0][:, HALF:], zeros)
        nc.vector.tensor_copy(windows[1][:, :HALF], zeros)
        nc.vector.tensor_copy(windows[2][:, :HALF], zeros)
        nc.vector.tensor_copy(windows[2][:, HALF:], zeros)

        scale_rows = w_scales.bitcast(I32).rearrange("e a q n -> q (e a) n")
        x_rows = xT.rearrange("(p j) w -> p j w", j=4)
        raws = [tile([P, T], F32, f"raw{j}") for j in range(4)]
        for j in (2, 0, 1, 3):
            nc.sync.dma_start(raws[j][:], x_rows[:, j, :])
            if j == 2:
                nc.sync.dma_start(offsets[:], offs)
        for quad in range(4):
            nc.sync.dma_start(
                first_plane[32 * quad : 32 * quad + 4].bitcast(I32), scale_rows[4 * quad : 4 * quad + 4, :2]
            )

        word_rows = w_words.bitcast(I32).rearrange("e a p b -> p (e a) b")
        first_words = tile([P, 2, 2 * BLOCK], U8, "first_words", "reused")
        nc.sync.dma_start(
            first_words[:].rearrange("p e b -> p (e b)").bitcast(I32).rearrange("p (e b) -> p e b", e=2),
            word_rows[:, :2, : BLOCK // 2],
        )
        gates = tile([P, SLOTS], F32, "gates")
        nc.sync.dma_start(gates[:, :GROUP], gate[:P, :GROUP])
        early_words = tile([P, 2, 2 * BLOCK], U8, "early_words")
        nc.sync.dma_start(
            early_words[:].rearrange("p e b -> p (e b)").bitcast(I32).rearrange("p (e b) -> p e b", e=2),
            word_rows[:, :2, BLOCK // 2 :],
        )
        late_words = tile([P, E - 2, 2 * N], U8, "late_words")
        nc.sync.dma_start(
            late_words[:].rearrange("p e b -> p (e b)").bitcast(I32).rearrange("p (e b) -> p e b", e=E - 2),
            word_rows[:, 2:, :],
        )
        plane_words = wplane[:].rearrange("p e n -> p (e n)").bitcast(I32).rearrange("p (e n) -> p e n", e=E - 2)
        for quad in range(4):
            nc.sync.dma_start(plane_words[32 * quad : 32 * quad + 4], scale_rows[4 * quad : 4 * quad + 4, 2:])
        nc.sync.dma_start(gates[:, GROUP:], gate[:P, GROUP:])

        picked = tile([P, SLOTS, 4], BF16, "picked")

        def vector_gather(j, first, last):
            nc.vector.tensor_copy(picked[:, first:last, j], raws[j][:].indirect(listed(first, last)))

        for j in (2, 0, 1):
            vector_gather(j, 0, HEAD_SPLIT)
            nc.scalar.activation(picked[:, HEAD_SPLIT:, j], raws[j][:].indirect(listed(HEAD_SPLIT, SLOTS)), COPY)
        one = tile([P, 1], F32, "one", "raw2")
        nc.vector.memset(one[:], 1.0)
        vector_gather(3, LAST_FIRST, LAST_END)
        for first, last in ((0, C), (C, LAST_FIRST), (LAST_END, 2 * GROUP), (2 * GROUP, SLOTS)):
            nc.scalar.activation(picked[:, first:last, 3], raws[3][:].indirect(listed(first, last)), COPY, scale=one[:])

        codes = tile([P, SLOTS], U32, "codes")
        scales = [tile([P, GROUP], U8, f"scales{g}", "reused" if g == 2 else None) for g in range(3)]

        def quantise(first, last):
            nc.vector.quantize_mx(
                out=codes[:, first:last].bitcast(FP8X4),
                scales=scales[first // GROUP][:, first % GROUP : (last - 1) % GROUP + 1],
                in_=picked[:, first:last, :].rearrange("p s j -> p (s j)"),
            )

        def weights(e, t):
            if e > 1:
                return late_words[:, e - 2, BLOCK * t : BLOCK * (t + 1)]
            return (first_words, early_words)[t // 2][:, e, BLOCK * (t % 2) : BLOCK * (t % 2 + 1)]

        def products(t, first, last, reader, backwards=False):
            bank = psum.tile([P, last - first], F32, name=reader)
            experts = range(first // C, (last - 1) // C + 1)
            for e in reversed(experts) if backwards else experts:
                low, high = max(first, C * e), min(last, C * (e + 1))
                plane = first_plane[:, e, :] if e < 2 else wplane[:, e - 2, :]
                nc.tensor.matmul_mx(
                    out=bank[:, low - first : high - first],
                    lhsT=weights(e, t).bitcast(FP4X4),
                    lhsT_scale=plane[:, P * t : P * (t + 1)],
                    rhs=codes[:, low:high].bitcast(FP8X4),
                    rhs_scale=scales[low // GROUP][:, low % GROUP : (high - 1) % GROUP + 1],
                    start=True,
                    stop=True,
                )
            return bank

        values = [tile([P, SLOTS], F32, f"values{t}") for t in range(NT)]

        def gated(t, first, last, backwards=False):
            bank = products(t, first, last, "vector", backwards)
            nc.vector.tensor_tensor(values[t][:, first:last], bank[:], gates[:, first:last], MULT)

        def vector_copy(t, first, last, backwards=False):
            nc.vector.tensor_copy(values[t][:, first:last], products(t, first, last, "vector", backwards)[:])

        def scalar_copy(t, first, last, backwards=False):
            nc.scalar.copy(values[t][:, first:last], products(t, first, last, "scalar", backwards)[:])

        def scalar_scatter(t, first, last):
            nc.scalar.activation(
                windows[t][:].indirect(listed(first, last)), values[t][:, first:last], COPY, scale=one[:]
            )

        def vector_scatter(t, first, last):
            nc.vector.tensor_tensor(
                windows[t][:].indirect(listed(first, last)), values[t][:, first:last], gates[:, first:last], MULT
            )

        quantise(0, C)
        quantise(C, GROUP)
        quantise(GROUP, 2 * GROUP)
        gated(0, 0, GROUP)
        vector_copy(1, 0, GROUP, True)
        quantise(2 * GROUP, SLOTS)
        windows.append(tile([P, T], F32, "window3", "picked"))
        nc.gpsimd.memset(windows[3][:], 0.0)
        gated(2, 0, GROUP, True)
        scalar_scatter(0, 0, GROUP)
        vector_scatter(1, 0, GROUP)
        scalar_copy(3, 0, GROUP, True)
        scalar_copy(1, GROUP, 2 * GROUP)
        scalar_copy(3, GROUP, 2 * GROUP)
        scalar_copy(1, 2 * GROUP, COPY_SPLIT)
        scalar_scatter(2, 0, GROUP)
        for t in (0, 2):
            for first in (GROUP, 2 * GROUP):
                gated(t, first, first + GROUP)
        vector_copy(3, 2 * GROUP, SLOTS)
        vector_copy(1, COPY_SPLIT, SLOTS)
        vector_scatter(3, 2 * GROUP, SLOTS)
        scalar_scatter(0, GROUP, SLOTS)
        nc.sync.dma_start(out[:P, :], windows[0][:])
        vector_scatter(1, GROUP, SLOTS)
        nc.sync.dma_start(out[P : 2 * P, :], windows[1][:])
        scalar_scatter(2, GROUP, SLOTS)
        nc.scalar.dma_start(out[2 * P : 3 * P, :HALF], windows[2][:, :HALF])
        nc.sync.dma_start(out[2 * P : 3 * P, HALF:], windows[2][:, HALF:])
        vector_scatter(3, 0, 2 * GROUP)
        nc.sync.dma_start(out[3 * P :, :HALF], windows[3][:, :HALF])
        nc.scalar.dma_start(out[3 * P :, HALF:], windows[3][:, HALF:])
